import numpy as np, ml_dtypes
CORES = [40,64,80,88,96,104,120,144]
N = 8
BF = ml_dtypes.bfloat16
def gentries(a):
    return np.ascontiguousarray(a.reshape(8, 16, -1).transpose(0, 2, 1)).reshape(8, -1)
def gtable(e):
    e = np.asarray(e); return np.ascontiguousarray(e.reshape(8, -1, 16).transpose(0, 2, 1)).reshape(128, -1).astype(np.int32)
W, NB, P, Q, RO, ST, LO, HI, OWN = 4096, 512, 256, 16, 3, 1, 4, 9, 0
def sites(rng):
    b = np.argsort(rng.random((N, 8, NB)), axis=-1); o = np.argsort(rng.random((N, 8, NB)), axis=-1)
    return b, np.ascontiguousarray(o[..., :P]), np.take_along_axis(b, o[..., P:], -1)
def some(rng):
    x = rng.integers(0, 256, (N, 8, 16, W), dtype=np.int16); c = rng.integers(0, W, (N, 8, 16, NB))
    pf = rng.integers(0, 256, (N, 8, 16, P)); pn = rng.integers(0, 256, (N, 8, 16, P))
    th = (rng.choice(np.array([1, 60, 400]), (N, 8, 1)) * rng.random((N, 8, 16))).astype(np.int64)
    return x, c, pf, pn, th
def lay(b, fl, nu, ca, ch):
    c = np.zeros((N, 8, 16, NB), np.int64); a = np.take_along_axis(b, fl, -1)
    np.put_along_axis(c, a[:, :, None, :], ca, 3); np.put_along_axis(c, nu[:, :, None, :], ch, 3)
    return c
def pack(x, c, b, fl, nu, pf, pn, th):
    return {"xf": x.reshape(N, 128, W).astype(np.float32).astype(BF), "cb": np.ascontiguousarray(c.reshape(N, 128, NB)).astype(np.int32), "bs": np.stack([gtable(v) for v in b]),
            "fs": np.stack([gtable(v) for v in fl]), "nb": np.stack([gtable(v) for v in nu]), "pf": pf.reshape(N, 128, P).astype(np.float32).astype(BF),
            "pn": pn.reshape(N, 128, P).astype(np.float32).astype(BF), "th": np.ascontiguousarray(th.reshape(N, 128, 1)).astype(np.int32)}
def setup_inputs(rng):
    b, fl, nu = sites(rng); x, c, pf, pn, th = some(rng)
    return pack(x, c, b, fl, nu, pf, pn, th)
def setup_inputs_corners(rng):
    b, fl, nu = sites(rng)
    for q in range(N):
        for g in range(8):
            if g in (0, 3): b[q, g] = np.arange(NB)
            if g == 1: b[q, g] = np.arange(NB)[::-1]
            o = np.concatenate([fl[q, g], np.setdiff1d(np.arange(NB), fl[q, g])])
            if g == 2: o = np.concatenate([np.arange(0, NB, 2), rng.permutation(np.arange(1, NB, 2))])
            if g == 3: o = np.arange(NB)
            if g == 4: o = np.arange(NB)[::-1]
            if g == 5: o = np.concatenate([rng.permutation(P), P + rng.permutation(P)])
            fl[q, g] = o[:P]; nu[q, g] = b[q, g][o[P:]]
    order = np.argsort(rng.random((N, 8, W)), axis=-1)
    order[:, 6:] = order[0, 6:].copy()
    tot = np.concatenate([np.broadcast_to(np.arange(4081), (N, 8, 4081)), rng.integers(0, 4081, (N, 8, W - 4081))], axis=2)
    sg = np.zeros((N, 8, W), np.int64); np.put_along_axis(sg, order, tot, 2); sg = sg[:, :, None, :]
    ln = (np.arange(16)[:, None] + np.arange(W)[None, :]) % 16
    x = (sg // 16 + (ln[None, None] < sg % 16)).astype(np.int16); loc = order[:, :, None, :4081]
    th = rng.choice(np.array([0, 1, 2, 7, 300, 1001, 4095, 4096, 6001, 8158, 8159]), (N, 8, 16)); th[:, 6:] = rng.integers(1002, 4160, (N, 2, 16))
    want = rng.choice(np.array([0, LO, LO + 1, HI - 1, HI, 16]), (N, 8, P))
    for q in range(N):
        for g in range(8):
            m = (g + q) % 8
            if m < 4: want[q, g] = rng.choice(np.array(((HI, 16), (0, LO), (LO + 1, HI - 1), (16, 16))[m]), P)
    sw = np.argsort(np.argsort(rng.random((N, 8, 16, P)), axis=2), axis=2) < want[:, :, None, :]
    d = th[..., None] // 2 + sw; lo = (rng.random((N, 8, 16, P)) * (4081 - d)).astype(np.int64)
    ch = np.take_along_axis(loc, lo + d, 3); cl = np.take_along_axis(loc, lo, 3)
    u = rng.integers(0, 2, (N, 8, 1, P)); z = np.zeros((N, 8, 16, P), np.int64)
    ca = np.where(u == 0, ch, cl); cc = np.where(u == 0, cl, ch)
    mv = rng.random(P) < 0.5; mv[0] = True; mv[P - 1] = False
    u[:, 6, 0] = np.where(mv, rng.integers(0, 2, P), np.arange(N)[:, None] % 2); u[:, 7] = rng.integers(0, 2)
    for g in (6, 7):
        small, large = [w[(w & (min(Q, 16) - 1)) > 0] for w in (order[0, g, :1001], order[0, g, 3080:4081])]
        small = rng.choice(small, (N, 16, P)); large = rng.choice(large, (N, 16, P)); up = u[:, g] == 0
        if g == 6: up = up != mv
        ca[:, g] = np.where(up, large, small); cc[:, g] = np.where(up, small, large)
    return pack(x, lay(b, fl, nu, ca, cc), b, fl, nu, z + 255 * u, z + 255 * (1 - u), th)
def setup_inputs_ends(rng):
    o = 1 + np.argsort(rng.random((N, 8, NB - 2)), axis=-1); k = 1 + np.argsort(rng.random((N, 8, NB - 2)), axis=-1)
    z = np.zeros((N, 8, 1), np.int64); fl = np.concatenate([z, o[..., :P - 2], z + NB - 1], axis=2); nu = np.concatenate([z, k[..., :P - 2], z + NB - 1], axis=2)
    b = np.zeros((N, 8, NB), np.int64); np.put_along_axis(b, fl, k[..., P - 2:], 2); np.put_along_axis(b, o[..., P - 2:], nu, 2)
    rk = 1 + np.argsort(rng.random((N, 8, W - 2)), axis=-1); n = 2 * W // 5; low = rk[:, :, None, :n]; high = rk[:, :, None, n:2 * n]
    x = rng.integers(0, 2, (N, 8, 16, W), dtype=np.int16) * np.int16(255)
    np.put_along_axis(x, low, 0, 3); np.put_along_axis(x, high, 255, 3)
    e = rng.integers(0, 2, (N, 8)); e[N - 1, 7] = 0
    x[..., 0] = 255 * e[:, :, None]; x[..., W - 1] = 255 * (1 - e)[:, :, None]
    eh = np.where(e == 1, 0, W - 1)[:, :, None, None]; el = W - 1 - eh; sh = (N, 8, 16, P)
    ch = np.where(rng.random(sh) < 0.75, eh, np.take_along_axis(high, rng.integers(0, n, sh), 3))
    cl = np.where(rng.random(sh) < 0.75, el, np.take_along_axis(low, rng.integers(0, n, sh), 3))
    u = rng.choice(np.array([0, 0, 1, 1, 2]), (N, 8, 1, P)); u[0] = rng.integers(0, 2, (8, 1, P)); u[N - 1] = rng.integers(0, 2, (8, 1, P)); u[N - 1, 7, 0, P - 1] = 0
    pf = np.where(u == 0, 0, np.where(u == 1, 255, 255 * rng.integers(0, 2, sh))); pn = np.where(u == 0, 255, np.where(u == 1, 0, 255 * rng.integers(0, 2, sh)))
    th = 8159 * rng.integers(0, 2, (N, 8, 16)); th[:, 0, 0] = 0; th[:, 7, 15] = 8159
    w = rng.choice(np.array([0.0, 0.3, 0.6, 0.8, 1.0]), (N, 8, 1, P)); w[0] = 0.0; w[N - 1] = 1.0
    up = (rng.random(sh) < w) == (u == 0); ca = np.where(up, ch, cl); cc = np.where(up, cl, ch)
    tie = rng.random(sh) < 0.1; tie[0] = False; tie[N - 1] = False
    return pack(x, lay(b, fl, nu, ca, np.where(tie, ca, cc)), b, fl, nu, pf, pn, th)
def setup_inputs_fresh(rng):
    b, fl, nu = sites(rng); x, c, pf, pn, th = some(rng); sh = (N, 8, 16, NB)
    sm = np.add.reduce(pf, axis=2); i = rng.integers(0, P, sh); r = np.arange(N)[:, None, None, None]; g = np.arange(8)[None, :, None, None]
    q = (r + ST * rng.integers(0, RO, sh)) % N
    c = np.where(rng.random(sh) < 0.9, Q * i + ((sm[q, g, i] + rng.integers(3, 11, sh)) & (Q - 1)), c)
    return pack(x, c, b, fl, nu, pf, pn, th)
def setup_inputs_spread(rng):
    b, fl, nu = sites(rng)
    x = np.minimum(np.exp2(8.01 * rng.random((N, 8, 1, W), dtype=np.float32)) * rng.random((N, 8, 16, W), dtype=np.float32), 255).astype(np.int16)
    pf = np.minimum(np.exp2(2 + 6.01 * rng.random((N, 8, 1, P))) * rng.random((N, 8, 16, P)), 255).astype(np.int64)
    pn = np.minimum(np.exp2(2 + 6.01 * rng.random((N, 8, 1, P))) * rng.random((N, 8, 16, P)), 255).astype(np.int64)
    c = np.minimum((W * rng.random((N, 8, 16, NB)) ** 3).astype(np.int64), W - 1); c = np.where(rng.random((N, 8, 1, NB)) < 0.5, c, W - 1 - c)
    kind = rng.choice(np.array([0.25, 0.25, 0.5, 1.0]), (N, 8, 1))
    th = np.minimum(np.exp2(13 * kind * rng.random((N, 8, 16))).astype(np.int64) - 1, 8159)
    return pack(x, c, b, fl, nu, pf, pn, th)
def check_inputs(d):
    bad = []
    for k, lo, hi in (("xf", 0, 255), ("cb", 0, W - 1), ("bs", 0, NB - 1), ("fs", 0, NB - 1), ("nb", 0, NB - 1), ("pf", 0, 255), ("pn", 0, 255), ("th", 0, 8159)):
        v = np.asarray(d[k]).astype(np.float32)
        if not (np.all(v >= lo) and np.all(v <= hi)): bad.append("range of " + k)
        elif np.any(v != np.floor(v)): bad.append("whole numbers of " + k)
    b, fl, nu = [np.stack([gentries(np.clip(np.asarray(v), 0, NB - 1).astype(np.int64)) for v in d[k]]) for k in ("bs", "fs", "nb")]
    if np.any(np.sort(b, axis=-1) != np.arange(NB)): bad.append("bs: a permutation of the boxes in every group")
    if np.any(np.sort(np.concatenate([np.take_along_axis(b, fl, -1), nu], axis=2), axis=-1) != np.arange(NB)): bad.append("fs, nb: the flyers' boxes and the nurses' boxes are all boxes, each once")
    return bad
def reference(xf, cb, bs, fs, nb, pf, pn, th):
    x = xf.astype(np.float32).astype(np.int32).reshape(N, 8, 16, W); c = cb.astype(np.int64).reshape(N, 8, 16, NB)
    b, fl, nu = [np.stack([gentries(v) for v in k]).astype(np.int64) for k in (bs, fs, nb)]
    rf = pf.astype(np.float32).astype(np.int32).reshape(N, 8, 16, P); rn = pn.astype(np.float32).astype(np.int32).reshape(N, 8, 16, P); lim = th.astype(np.int64).reshape(N, 8, 16, 1)
    for t in range(RO):
        for r in range(N):
            q = (r + ST * t) % N
            box = np.take_along_axis(b[r], fl[r], 1); nur = nu[r].copy()
            ca = np.take_along_axis(c[r], box[:, None, :], 2); ch = np.take_along_axis(c[r], nur[:, None, :], 2)
            xa = np.take_along_axis(x[q], ca.reshape(8, 1, 16 * P), 2).reshape(8, 16, 16, P)
            xh = np.take_along_axis(x[q], ch.reshape(8, 1, 16 * P), 2).reshape(8, 16, 16, P)
            u = rf[q][:, :, None, :]; v = rn[q][:, :, None, :]
            score = np.add.reduce(np.abs(xa - u) + np.abs(xh - v) - np.abs(xh - u) - np.abs(xa - v), axis=1)
            sw = score > lim[q]; s = np.add.reduce(sw.astype(np.int64), axis=1)
            np.put_along_axis(c[r], box[:, None, :], np.where(sw, ch, ca), 2); np.put_along_axis(c[r], nur[:, None, :], np.where(sw, ca, ch), 2)
            flag = np.zeros((8, NB), bool); np.put_along_axis(flag, fl[r], s >= HI, 1)
            inv = np.argsort(b[r], axis=1); turn = s <= LO
            fl[r] = np.where(turn, np.take_along_axis(inv, nur, 1), fl[r]); nu[r] = np.where(turn, box, nur)
            total = np.add.reduce(s, axis=1)[:, None]
            if not OWN: total = np.zeros((8, 1), np.int64) + np.add.reduce(total, axis=None)
            mate = np.arange(NB)[None, :] ^ ((total & (NB - 1)) | 1)
            both = flag & np.take_along_axis(flag, mate, 1)
            b[r] = np.where(both, np.take_along_axis(b[r], mate, 1), b[r])
            col = Q * np.arange(P)[None, :] + ((np.add.reduce(rf[q].astype(np.int64), axis=1) + s) & (Q - 1))
            np.put_along_axis(x[q], col[:, None, :], rf[q], 2)
    who = [(q - ST * (RO - 1)) % N for q in range(N)]
    return {"yc": c[who].reshape(N, 128, NB).astype(np.float32), "yb": np.stack([gtable(b[r]) for r in who]).astype(np.float32),
            "yf": np.stack([gtable(fl[r]) for r in who]).astype(np.float32), "yn": np.stack([gtable(nu[r]) for r in who]).astype(np.float32)}

@@ -1,0 +1,583 @@
+from concourse.mybir import AluOpType as OP, AxisListType, ActivationFunctionType as AF
+
+P, WX, RO = 256, 4096, 3
+CH = [(0, 64), (64, 128), (128, 192), (192, 256)]
+AH = [(0, 128), (128, 256)]
+NE = 8
+FRAC = -0.5 + 2.0 ** -10
+CY, GA, SC, PE, WK, HOP = 0.00083, 1.56, 3.8, 0.00046, 0.15, 7.0
+
+SCRATCH = {}
+
+
+def _sb(name, cols, dtype="float32"):
+    SCRATCH[name] = ("sbuf", [128, cols], dtype)
+
+
+for _n, _c, _d in [
+        ("X", WX, "bfloat16"), ("CBI", 512, "int32"), ("BSI", 32, "int32"), ("FSI", 16, "int32"), ("NBI", 16, "int32"), ("THI", 1, "int32"),
+        ("PFB", 256, "bfloat16"), ("PNB", 256, "bfloat16"), ("LU0", 64, "uint16"), ("CS", 512, "int32"),
+        ("CF", 4096, "bfloat16"), ("CN", 4096, "bfloat16"), ("GH", 4096, "bfloat16"), ("GA", 4096, "bfloat16"),
+        ("OHF", 4096, "bfloat16"), ("OHN", 4096, "bfloat16"), ("OAF", 4096, "bfloat16"), ("OAN", 4096, "bfloat16"),
+        ("KHF", 256, "bfloat16"), ("KHN", 256, "bfloat16"), ("KAF", 256, "bfloat16"), ("KAN", 256, "bfloat16"),
+        ("SEL", 2064, "bfloat16"), ("NSEL", 2064, "bfloat16"), ("ONE", 128, "bfloat16"), ("BLK0", 128, "bfloat16"), ("BLK", 128, "bfloat16"),
+        ("IDN", 128, "bfloat16"), ("ONF", 128, "float32"), ("BLKF", 128, "float32"),
+        ("M16", 128, "float32"), ("MB0", 128, "float32"), ("M16B", 128, "float32"), ("IC16", 32, "float32"), ("VC", 32, "bfloat16"), ("VLO", 32, "bfloat16"),
+        ("IOV", 512, "float32"), ("DM", 32, "float32"),
+        ("LBI", 128, "int32"), ("LBJ", 128, "int32"), ("LP", 128, "bfloat16"), ("RBI", 32, "int32"), ("RBJ", 32, "int32"), ("RP", 32, "bfloat16"),
+        ("E15", 16, "float32"), ("INV", 512, "float32"), ("GROW", 256, "float16"), ("BROW", 512, "float32"), ("EF", 512, "float32"),
+        ("AROW", 256, "float16"), ("NROW", 256, "float16"), ("AL", 16, "uint16"), ("NL", 16, "uint16"), ("ALF", 16, "float32"), ("NLF", 16, "float32"),
+        ("SW", 256, "bfloat16"), ("RS", 8, "float32"), ("HN", 256, "float32"), ("AN", 256, "float32"), ("AM", 256, "float32"), ("V", 256, "float32"), ("U", 256, "float32"),
+        ("LH", 128, "bfloat16"), ("XL", 32, "uint16"), ("XI", 32, "int32"), ("XJ", 32, "int32"),
+        ("PM", 128, "bfloat16"), ("XM", 32, "float32"), ("HL", 8, "float32"), ("HLU", 2, "uint16"),
+        ("AX", 512, "float32"), ("WI", 256, "int32"), ("WJ", 256, "int32"), ("VB", 512, "bfloat16"), ("VLB", 64, "float32"), ("GXL", 64, "float16"),
+        ("BO", 32, "float32"), ("BD", 32, "float32"), ("TL", 16, "float32"), ("DFG", 16, "float32"), ("TD", 16, "float32"), ("DAN", 16, "float32"), ("TA", 16, "float32"),
+        ("XC", 16, "uint16"), ("XDF", 256, "float32"), ("FLG", 256, "bfloat16"),
+        ("YC", 512, "float32"), ("YB", 32, "float32"), ("YF", 16, "float32"), ("YN", 16, "float32"),
+        ("VW0", 512, "float32"), ("VW1", 512, "float32"), ("VF", 512, "bfloat16"), ("DL0", 64, "float32"), ("DR0", 64, "float32"), ("LE0", 64, "float32"),
+        ("AF", 256, "float32"), ("HF", 256, "float32"), ("DD", 256, "float32"), ("AMF", 256, "float32")]:
+    _sb(_n, _c, _d)
+for _t in range(RO):
+    for _n, _c, _d in [("AU", 256, "uint16"), ("HU", 256, "uint16"), ("LS", 64, "float32"), ("FU", 32, "uint16")]:
+        _sb(_n + str(_t), _c, _d)
+    if _t < RO - 1:
+        for _n, _c, _d in [("AS", 256, "uint16"), ("HS", 256, "uint16"), ("LO", 64, "float32")]:
+            _sb(_n + str(_t), _c, _d)
+ALIAS = {}
+for _k, _d, _l in (("KF", "float32", [(n, 1) for n in "PL PL16 PW PWS ADS P2 NP2 TH2 HBF XKF".split()]),
+                   ("KI", "int32", [(n, 16) for n in "EI EJ UI UJ UK IL16".split()] + [(n, 1) for n in "PI PJ HBI HBJ XK".split()])):
+    _o = 0
+    for _n, _w in _l:
+        ALIAS[_n] = (_k, _o, _w)
+        _o += _w
+    _sb(_k, _o, _d)
+PS = ["Z0", "Z1", "Z2", "Z3", "VT", "PF", "SLB", "RL"]
+for _n in PS:
+    SCRATCH[_n] = ("psum", [128, 512], "float32")
+
+MSGS = [("mE", "LS0", "LE0", 0, 64)]
+for _t in range(RO - 1):
+    MSGS += [("mH%d_%d" % (_t, _c), "HS%d" % _t, "HU%d" % (_t + 1), _a, _b) for _c, (_a, _b) in enumerate(CH)]
+    MSGS += [("mA%d_%d" % (_t, _c), "AS%d" % _t, "AU%d" % (_t + 1), _a, _b) for _c, (_a, _b) in enumerate(AH)]
+    MSGS += [("mL%d" % _t, "DL0" if _t == 0 else "LO%d" % _t, "DR0" if _t == 0 else "LS%d" % (_t + 1), 0, 64)]
+LOADS = ["NBI", "CBI", "BSI", "FSI", "THI", "PFB", "PNB", "X"]
+OUTS = ["yc", "yb", "yf", "yn"]
+SEMAPHORES = ["sv", "ss", "sp", "sg", "loc"] + [m[0] for m in MSGS] + ["d" + n for n in LOADS + OUTS]
+
+
+def hop(core, dst, topo, T):
+    if topo.may_write(core, dst):
+        return core
+    own = [c for c in topo.cores_of(core) if T.rank_of(c) is None and topo.may_write(c, dst)]
+    return [c for c in own if topo.die(c) == topo.die(core)][0]
+
+
+def mask_of(src, dst, topo):
+    m = 0
+    for e in topo.engines(src, dst)[:NE]:
+        m |= 1 << e
+    return m
+
+
+def put(g, T, topo, src, dst, out, in_, sem):
+    rid, pid = topo.addr(dst, src)
+    g.remote_dma(out_ap=out, in_ap=in_, remote_sem=T.sem[sem], local_sem=T.sem.loc, pid=pid, routing_id=rid, dma_engine_mask=mask_of(src, dst, topo))
+
+
+def relay_program(g, core, T, topo):
+    for r, c in enumerate(T.cores):
+        dst = T.cores[(r + 1) % len(T.cores)]
+        if c in topo.cores_of(core) and hop(c, dst, topo, T) == core:
+            for sem, _, land, a, b in MSGS:
+                g.wait_ge(T.sem[sem], NE)
+                put(g, T, topo, core, dst, T[land][:, a:b], T[land][:, a:b], sem)
+            g.wait_ge(T.sem.loc, NE * len(MSGS))
+
+
+def arrange(ops):
+    n = len(ops)
+    pred = [set(o["after"]) for o in ops]
+    hist = {}
+    for i, o in enumerate(ops):
+        for group, w in ((o["rd"], False), (o["wr"], True)):
+            for name, lo, hi in group:
+                for j, jlo, jhi, jw in hist.get(name, []):
+                    if j != i and jlo < hi and lo < jhi and (w or jw):
+                        pred[i].add(j)
+        for group, w in ((o["rd"], False), (o["wr"], True)):
+            for name, lo, hi in group:
+                old = hist.get(name, [])
+                if w:
+                    old = [r for r in old if not (r[1] >= lo and r[2] <= hi)]
+                hist[name] = old + [(i, lo, hi, w)]
+    succ = [[] for _ in ops]
+    for i in range(n):
+        for j in pred[i]:
+            succ[j].append(i)
+    rank = [0.0] * n
+    for i in range(n - 1, -1, -1):
+        rank[i] = ops[i]["cost"] + max([rank[j] + WK for j in succ[i]] + [0.0])
+    left = [len(p) for p in pred]
+    ready = [0.0] * n
+    free = {}
+    avail = [i for i in range(n) if left[i] == 0]
+    order = []
+    while avail:
+        best = None
+        for i in avail:
+            o = ops[i]
+            st = max(free.get(o["q"], 0.0), ready[i]) if o["q"] != "r" else ready[i]
+            key = (st - (0.02 * min(rank[i], 60.0)), -rank[i], i)
+            if best is None or key < best[0]:
+                best = (key, i, st)
+        _, i, st = best
+        avail.remove(i)
+        end = st + ops[i]["cost"]
+        if ops[i]["q"] != "r":
+            free[ops[i]["q"]] = st + ops[i]["hold"]
+        order.append((st, len(order), i))
+        for j in succ[i]:
+            left[j] -= 1
+            ready[j] = max(ready[j], end + WK)
+            if left[j] == 0:
+                avail.append(j)
+    return [ops[i] for _, _, i in order]
+
+
+def rank_program(g, core, T, topo):
+    rank = T.rank_of(core)
+    if rank is None:
+        relay_program(g, core, T, topo)
+        return
+    nxt = T.cores[(rank + 1) % len(T.cores)]
+    via = hop(core, nxt, topo, T)
+
+    Q = {"v": g.vector, "s": g.scalar, "p": g.tensor, "g": g, "y": g.sync}
+    QS = {"v": "sv", "s": "ss", "p": "sp", "g": "sg"}
+    cnt = {"sv": 0, "ss": 0, "sp": 0, "sg": 0}
+    known = {q: {} for q in Q}
+    acc = {}
+    total = {}
+    ops = []
+    index = {}
+
+    def wait(q, sem, val, know):
+        k = known[q]
+        if k.get(sem, 0) < val:
+            Q[q].wait_ge(T.sem[sem], val)
+            k[sem] = val
+            for s2, v2 in know.items():
+                if k.get(s2, 0) < v2:
+                    k[s2] = v2
+
+    def deps(q, reads, writes, dma=False):
+        need = {}
+        for group, w in ((reads, False), (writes, True)):
+            for name, lo, hi in group:
+                ps = name in PS
+                for r in acc.get(name, []):
+                    same = r[3] == q and not r[6] and not dma
+                    if (r[0] >= hi or r[1] <= lo) and (same or not ps):
+                        continue
+                    if not (w or r[2] or (ps and not same)):
+                        continue
+                    if same and q == "p":
+                        continue
+                    if r[4] not in need or need[r[4]][0] < r[5]:
+                        need[r[4]] = (r[5], r[7])
+        for sem in sorted(need, key=lambda s: -len(need[s][1])):
+            wait(q, sem, need[sem][0], need[sem][1])
+
+    def note(q, reads, writes, sem, val, dma):
+        know = dict(known[q])
+        for group, w in ((reads, False), (writes, True)):
+            for name, lo, hi in group:
+                old = acc.get(name, [])
+                if name in PS:
+                    keep = [r for r in old if r[3] == q and not (r[0] >= lo and r[1] <= hi and (w or not r[2]))]
+                elif w:
+                    keep = [r for r in old if not (r[0] >= lo and r[1] <= hi)]
+                else:
+                    keep = [r for r in old if not (r[0] >= lo and r[1] <= hi and r[3] == q and not r[2] and not r[6] and not dma)]
+                acc[name] = keep + [(lo, hi, w, q, sem, val, dma, know)]
+
+    def add(kind, q, fns, rd, wr, cost, hold=None, after=(), extra=None):
+        ops.append({"kind": kind, "q": q, "fns": fns, "rd": rd, "wr": wr, "cost": cost, "hold": cost if hold is None else hold, "after": after, "extra": extra})
+        return len(ops) - 1
+
+    def do(q, fns, rd, wr, cost):
+        return add("do", q, fns if isinstance(fns, list) else [fns], rd, wr, cost)
+
+    def dma(q, out, in_, name, rd, wr, size):
+        add("dma", q, [lambda e: e.dma_start(out=out, in_=in_)], rd, wr, 2.0 + size / 220e3, 0.1, (), "d" + name)
+
+    def send(sem):
+        _, src, land, a, b = [m for m in MSGS if m[0] == sem][0]
+        i = add("send", "g", None, [(src, a, b)], [("SENDQ", 0, 1)], 1.0, 1.0, (), sem)
+        add("land", "r", None, [], [(land, a, b)], HOP, 0.0, (i,), sem)
+
+    def issue(o):
+        q = o["q"]
+        if o["kind"] == "do":
+            deps(q, o["rd"], o["wr"])
+            for fn in o["fns"]:
+                cnt[QS[q]] += 1
+                fn(Q[q]).then_inc(T.sem[QS[q]], 1)
+            note(q, o["rd"], o["wr"], QS[q], cnt[QS[q]], False)
+        elif o["kind"] == "dma":
+            deps(q, o["rd"], o["wr"], True)
+            o["fns"][0](Q[q]).then_inc(T.sem[o["extra"]], 16)
+            total[o["extra"]] = 16
+            note(q, o["rd"], o["wr"], o["extra"], 16, True)
+        elif o["kind"] == "send":
+            m = [m for m in MSGS if m[0] == o["extra"]][0]
+            deps("g", o["rd"], [])
+            dst, out = (nxt, m[2]) if via == core else (via, m[2])
+            put(g, T, topo, core, dst, T[out][:, m[3]:m[4]], T[m[1]][:, m[3]:m[4]], m[0])
+        else:
+            land, a, b = o["wr"][0]
+            acc.setdefault(land, []).append((a, b, True, "r", o["extra"], NE, True, {}))
+            total[o["extra"]] = NE
+
+    def rg(name, a=0, b=None):
+        if name in ALIAS:
+            k, o, w = ALIAS[name]
+            return (k, o + a, o + (w if b is None else b))
+        return (name, a, SCRATCH[name][1][1] if b is None else b)
+
+    def ap(x):
+        return T[x[0]][:, x[1]:x[2]]
+
+    def two(x):
+        return SCRATCH[x[0]][0] == "sbuf" and SCRATCH[x[0]][2] in ("bfloat16", "float16", "uint16")
+
+    def el(n, f=1.0):
+        return max(64, n * f) * CY
+
+    def tt(o, x, y, op):
+        f = 1.0 if x[0] in PS or y[0] in PS else 2.0
+        do("v", lambda e: e.tensor_tensor(out=ap(o), in0=ap(x), in1=ap(y), op=op), [x, y], [o], el(o[2] - o[1], f))
+
+    def ts(o, x, s1, op0, s2=None, op1=None):
+        rd = [x] + [s for s in (s1, s2) if isinstance(s, tuple)]
+        a1 = ap(s1) if isinstance(s1, tuple) else s1
+        a2 = ap(s2) if isinstance(s2, tuple) else s2
+        c = el(o[2] - o[1], 0.5 if two(o) and two(x) else 1.0)
+        if op1 is None:
+            do("v", lambda e: e.tensor_scalar(out=ap(o), in0=ap(x), scalar1=a1, scalar2=None, op0=op0), rd, [o], c)
+        else:
+            do("v", lambda e: e.tensor_scalar(out=ap(o), in0=ap(x), scalar1=a1, scalar2=a2, op0=op0, op1=op1), rd, [o], c)
+
+    def cp(o, x, out=None, in_=None):
+        w, r = out if out is not None else ap(o), in_ if in_ is not None else ap(x)
+        do("v", lambda e: e.tensor_copy(out=w, in_=r), [x], [o], el(max(x[2] - x[1], o[2] - o[1]) if out is None else 256, 0.5 if two(o) and two(x) else 1.0))
+
+    def act(out, in_, rd, wr, n, scale=1.0):
+        do("s", lambda e: e.activation(out, in_, AF.Copy, scale=scale), rd, wr, n * CY + 0.05)
+
+    def fill(o, c):
+        do("v", lambda e: e.memset(ap(o), c), [], [o], el(o[2] - o[1], 0.5 if two(o) else 1.0))
+
+    def gat(o, win, off):
+        do("v", lambda e: e.tensor_copy(out=ap(o), in_=ap(win).indirect(ap(off))), [win, off], [o], 0.05 + (o[2] - o[1]) * GA * CY)
+
+    def sca(win, off, x):
+        do("v", lambda e: e.tensor_copy(out=ap(win).indirect(ap(off)), in_=ap(x)), [x, off], [win], 0.05 + (x[2] - x[1]) * SC * CY)
+
+    def mmf(o, l, r, start, stop, kp=128):
+        return lambda e: e.matmul(ap(o), T[l[0]][0:kp, l[1]:l[2]], T[r[0]][0:kp, r[1]:r[2]], start, stop)
+
+    def sel(neg, k):
+        return T["NSEL" if neg else "SEL"][:, 128 * k:128 * k + 128]
+
+    def rowlist(o, row, a, b):
+        def one(l):
+            return lambda e: e.matmul(ap(o), sel(0, l), T[row][:, a + l:b:16], l == 0, l == 15)
+        do("p", [one(l) for l in range(16)], [rg("SEL"), (row, a, b)], [o], 1024 * PE)
+
+    def aff(o, x, pat, op, fillv, base, cm):
+        do("g", lambda e: e.affine_select(ap(o), ap(x), pat, op, fillv, base, cm), [x], [o], 0.17 + 2 * (o[2] - o[1]) * CY)
+
+    def iota(o, pat, base, cm, flag=True):
+        do("g", (lambda e: e.iota(ap(o), pat, base, cm, allow_small_or_imprecise_dtypes=True)) if flag else (lambda e: e.iota(ap(o), pat, base, cm)),
+           [], [o], 0.13 + 2 * (o[2] - o[1]) * CY)
+
+    def start():
+        for q, n, src in (("y", "NBI", "nb"), ("y", "CBI", "cb"), ("s", "PFB", "pf"), ("s", "PNB", "pn"), ("y", "BSI", "bs"), ("y", "FSI", "fs"), ("y", "X", "xf"), ("s", "THI", "th")):
+            dma(q, T[n][:], T[src][:], n, [], [rg(n)], 128 * SCRATCH[n][1][1] * 3)
+        for n, c in (("ONE", 1.0), ("PW", 1.0), ("ADS", FRAC), ("SEL", 0.0), ("NSEL", 0.0)):
+            fill(rg(n), c)
+        aff(rg("BLK0"), rg("ONE"), [[-16, 8], [0, 16]], OP.is_ge, 0.0, 0, 1)
+        aff(rg("BLK"), rg("BLK0"), [[16, 8], [0, 16]], OP.is_ge, 0.0, 15, -1)
+        iota(rg("PI"), [[0, 1]], 0, 1, False)
+        iota(rg("M16"), [[0, 8], [1, 16]], 0, 0)
+        for m in range(8):
+            s0 = 16 * m
+            cp(("SEL", m, m + 1), rg("BLK"), T.SEL[:, s0:s0 + 129 * 15 + 1:129], T.BLK[:, s0:s0 + 16])
+            act(T.NSEL[:, s0:s0 + 129 * 15 + 1:129], T.BLK[:, s0:s0 + 16], [rg("BLK")], [("NSEL", m, m + 1)], 16, -1.0)
+        cp(rg("LU0", 48, 64), rg("NBI"))
+        gat(rg("HU0"), rg("CBI"), rg("LU0", 48, 64))
+        cp(rg("LU0", 0, 32), rg("BSI"))
+        gat(rg("CS"), rg("CBI"), rg("LU0", 0, 32))
+        cp(rg("LU0", 32, 48), rg("FSI"))
+        gat(rg("AU0"), rg("CS"), rg("LU0", 32, 48))
+        for k in range(16):
+            cp(("CF", k, k + 1), rg("PFB"), T.CF[:, k:4096:16], T.PFB[:, :])
+            if k < 8:
+                act(T.CN[:, k:4096:16], T.PNB[:, :], [rg("PNB")], [("CN", k, k + 1)], 256)
+            else:
+                cp(("CN", k, k + 1), rg("PNB"), T.CN[:, k:4096:16], T.PNB[:, :])
+        cp(rg("PF", 0, 256), rg("PFB"))
+        cp(rg("PF", 256, 512), rg("PNB"))
+        aff(rg("IDN"), rg("ONE"), [[-1, 128]], OP.is_equal, 0.0, 0, 1)
+        iota(rg("IC16"), [[16, 32]], 0, 0)
+        iota(rg("IOV"), [[1, 512]], 0, 0)
+        aff(rg("MB0"), rg("M16"), [[-16, 8], [0, 16]], OP.is_ge, 99.0, 0, 1)
+        aff(rg("M16B"), rg("MB0"), [[16, 8], [0, 16]], OP.is_ge, 99.0, 15, -1)
+        for b in range(1, 9):
+            aff(rg("PW"), rg("PW"), [[0, 1]], OP.not_equal, 2.0 ** -b, -b, 1)
+        aff(rg("PWS"), rg("PW"), [[0, 1]], OP.not_equal, 0.0, 0, 1)
+        aff(rg("ADS"), rg("ADS"), [[0, 1]], OP.not_equal, 1.0, 0, 1)
+        fill(rg("ONF"), 1.0)
+        ts(rg("PJ"), rg("PI"), 15, OP.bitwise_and)
+        cp(rg("PL"), rg("PJ"))
+        ts(rg("PL16"), rg("PL"), 16.0, OP.mult)
+        ts(rg("TH2"), rg("THI"), 0.5, OP.mult)
+        ts(rg("DM"), rg("M16", 0, 32), rg("PL"), OP.is_equal)
+        ts(rg("VLO"), rg("ONE", 0, 32), rg("PL"), OP.mult)
+        cp(rg("VC"), rg("IC16"))
+        ts(rg("IL16"), rg("IC16", 0, 16), 16.0, OP.mult, rg("PL16"), OP.add)
+        do("v", lambda e: e.reciprocal(ap(rg("P2")), ap(rg("PW"))), [rg("PW")], [rg("P2")], 0.2)
+        ts(rg("NP2"), rg("P2"), -2.0, OP.mult)
+        for bi, bj, src, o, n in (("LBI", "LBJ", "M16", "LP", 128), ("RBI", "RBJ", "IC16", "RP", 32)):
+            ts(rg(bi), rg(src, 0, n), rg("PW"), OP.mult, FRAC, OP.add)
+            ts(rg(bj), rg(bi), 1, OP.bitwise_and)
+            ts(rg(o), rg(bj), rg("NP2"), OP.mult, rg("P2"), OP.add)
+        cp(rg("BLKF"), rg("BLK"))
+        rowlist(rg("RL", 0, 16), "PFB", 0, 256)
+        cp(rg("EI"), rg("RL", 0, 16))
+        ts(rg("EJ"), rg("EI"), 15, OP.bitwise_and)
+        cp(rg("E15"), rg("EJ"))
+        fill(rg("VW0"), -16384.0)
+        fill(rg("VW1"), -16384.0)
+        fill(rg("VF"), 0.0)
+        cp(rg("LS0", 0, 16), rg("FSI"))
+        cp(rg("LS0", 32, 64), rg("BSI"))
+        sca(rg("INV"), rg("LU0", 0, 32), rg("IOV"))
+        gat(rg("GROW"), rg("INV"), rg("LU0", 48, 64))
+        rowlist(rg("RL", 16, 32), "GROW", 0, 256)
+        ts(rg("LS0", 16, 32), rg("RL", 16, 32), 0.0625, OP.mult)
+        send("mE")
+
+    def frames(role, t, a, b):
+        u = T[role + "U%d" % t][:, a:b]
+        o = ("G" + role, 16 * a, 16 * b)
+        do("s", lambda e: e.activation(ap(o), ap(rg("X")).indirect(u), AF.Copy), [rg("X"), rg(role + "U%d" % t, a, b)], [o], 0.065 + 16 * (b - a) * GA * CY)
+
+    def maxima(role, a, b):
+        gx = ("G" + role, 16 * a, 16 * b)
+        row0 = T["G" + role][:, 16 * a:16 * b:16]
+
+        def first(f, o):
+            k = ("K" + role + f, a, b)
+            do("v", lambda e: e.tensor_tensor(out=ap(k), in0=row0, in1=T.PF[:, o + a:o + b], op=OP.max), [gx, ("PF", o + a, o + b)], [k], el(b - a))
+
+        def rest(f, c):
+            o, d = ("O" + role + f, 16 * a, 16 * b), (c, 16 * a, 16 * b)
+            do("v", lambda e: e.tensor_tensor_scan(ap(o), ap(d), ap(gx), 255.0, OP.min, OP.max), [gx, rg(c)], [o], el(16 * (b - a), 0.5))
+        first("F", 0)
+        first("N", 256)
+        do("v", lambda e: e.memset(row0, 255.0), [], [gx], el(b - a))
+        rest("F", "CF")
+        rest("N", "CN")
+
+    def sums(role, c, a, b):
+        z = ("Z%d" % c, 0, b - a)
+
+        def one(f, k):
+            neg = (role == "H") == (f == "F")
+            rhs = T["O" + role + f][:, 16 * a + k:16 * b:16] if k else T["K" + role + f][:, a:b]
+            return lambda e: e.matmul(ap(z), sel(neg, k), rhs, role == "H" and f == "F" and k == 0, role == "A" and f == "N" and k == 15)
+        for f in ("F", "N"):
+            neg = (role == "H") == (f == "F")
+            do("p", [one(f, k) for k in range(16)], [rg("NSEL" if neg else "SEL"), ("O" + role + f, 16 * a, 16 * b), ("K" + role + f, a, b)],
+               [(z[0], 0, 512) if (role, f) == ("H", "F") else z], 16 * max(64, b - a) * PE)
+
+    def boxes_of_sites():
+        for l in range(16):
+            act(T.EF[:, l:512:16], T.LS2[:, 32:64], [rg("LS2", 32, 64), rg("DM")], [("EF", l, l + 1)], 32, T.DM[:, l:l + 1])
+        do("p", mmf(rg("RL", 0, 512), rg("BLKF"), rg("EF"), True, True), [rg("BLKF"), rg("EF")], [rg("RL", 0, 512)], 2048 * PE)
+        act(ap(rg("BROW")), ap(rg("RL", 0, 512)), [rg("RL")], [rg("BROW")], 512)
+        for off, row, u, f in ((0, "AROW", "AL", "ALF"), (16, "NROW", "NL", "NLF")):
+            gat(rg(row), rg("BROW"), rg("FU2", off, off + 16))
+            rowlist(rg("RL", off, off + 16), row, 0, 256)
+            ts(rg(f), rg("RL", off, off + 16), 0.0625, OP.mult)
+            cp(rg(u), rg(f))
+
+    def take(t):
+        cp(rg("HF"), rg("HU%d" % t))
+        cp(rg("AF"), rg("AU%d" % t))
+        tt(rg("DD"), rg("HF"), rg("AF"), OP.subtract)
+        if t < RO - 1:
+            ts(rg("AMF"), rg("AF"), -4096.0, OP.add)
+
+    def take_lists(t):
+        if t == 1:
+            tt(rg("LS1"), rg("LE0"), rg("DR0"), OP.add)
+        cp(rg("FU%d" % t), rg("LS%d" % t, 0, 32))
+
+    def decide(t, c):
+        a, b = CH[c]
+        n = b - a
+        z, sr = ("Z%d" % c, 0, n), ("Z%d" % c, 256, 256 + n)
+        sw = rg("SW", a, b)
+        f = rg("FU%d" % t, a // 16, b // 16)
+        ts(sw, z, rg("TH2"), OP.is_gt)
+        do("p", mmf(sr, rg("BLK"), sw, True, True), [rg("BLK"), sw], [sr], 64 * PE)
+        rowlist(("SLB", 16 * t + a // 16, 16 * t + b // 16), "SW", a, b)
+        do("v", lambda e: e.tensor_reduce(T.RS[:, c:c + 1], ap(sw), AxisListType.X, OP.add), [sw], [("RS", c, c + 1)], el(n))
+        if t < RO - 1:
+            o = 128 * (c % 2)
+            tu, xs, xd, y = [("VT", o + 256 * (i // 2) + 64 * (i % 2), o + 256 * (i // 2) + 64 * (i % 2) + n) for i in range(4)]
+            ts(tu, sr, 4.0, OP.is_le)
+            tt(xs, tu, sw, OP.not_equal)
+            tt(xd, xs, rg("DD", a, b), OP.mult)
+            tt(rg("HN", a, b), rg("HF", a, b), xd, OP.subtract)
+            cp(rg("HS%d" % t, a, b), rg("HN", a, b))
+            send("mH%d_%d" % (t, c))
+            tt(rg("AN", a, b), rg("AF", a, b), xd, OP.add)
+            ts(y, sr, 9.0, OP.is_lt, 8192.0, OP.mult)
+            tt(rg("V", a, b), rg("AN", a, b), y, OP.subtract)
+            sca(rg("VW%d" % t), f, rg("V", a, b))
+            tt(rg("AM", a, b), rg("AMF", a, b), xd, OP.add)
+            tt(rg("U", a, b), rg("AM", a, b), y, OP.add)
+        else:
+            ts(rg("FLG", a, b), sr, 9.0, OP.is_ge)
+            sca(rg("VF"), f, rg("FLG", a, b))
+            tt(rg("XDF", a, b), rg("SW", a, b), rg("DD", a, b), OP.mult)
+
+            def box(base, lst, op):
+                do("v", lambda e: e.tensor_tensor(out=ap(rg("YC")).indirect(T[lst][:, a // 16:b // 16]), in0=T[base][:, a:b], in1=T.XDF[:, a:b], op=op),
+                   [(base, a, b), rg("XDF", a, b), rg(lst)], [rg("YC")], 0.05 + n * SC * CY)
+            box("AF", "AL", OP.add)
+            box("HF", "NL", OP.subtract)
+
+    def store(t, a, b):
+        c, d = a // 16, b // 16
+        tt(rg("UI", c, d), ("SLB", 16 * t + c, 16 * t + d), rg("E15", c, d), OP.add)
+        ts(rg("UJ", c, d), rg("UI", c, d), 15, OP.bitwise_and)
+        tt(rg("UK", c, d), rg("UJ", c, d), rg("IL16", c, d), OP.add)
+        cp(rg("XC", c, d), rg("UK", c, d))
+        sca(rg("X"), rg("XC", c, d), rg("PFB", a, b))
+
+    def xor_list():
+        s, x = ("SLB", 64, 65), ("RL", 64, 96)
+        do("p", [mmf(s, rg("ONF"), ("RS", c, c + 1), c == 0, c == len(CH) - 1) for c in range(len(CH))], [rg("ONF"), ("RS", 0, len(CH))], [s], 1024 * PE)
+        ts(rg("HBI"), s, rg("PWS"), OP.mult, rg("ADS"), OP.add)
+        ts(rg("HBJ"), rg("HBI"), 1, OP.bitwise_and)
+        tt(rg("HBF"), rg("HBJ"), rg("PW"), OP.mult)
+        ts(rg("LH"), rg("LP"), rg("HBF"), OP.mult)
+        do("p", [mmf(x, rg("IDN"), rg("VC"), True, False), mmf(x, rg("IDN"), rg("VLO"), False, False), mmf(x, rg("LH"), rg("RP"), False, True, 9)],
+           [rg("IDN"), rg("VC"), rg("VLO"), rg("LH"), rg("RP")], [x], 192 * PE)
+        cp(rg("XL"), x)
+        cp(rg("XI"), x)
+
+    def partners(t):
+        gat(rg("AX"), rg("VW%d" % t), rg("XL"))
+
+        def half(a, b):
+            o = rg("WI", a, b)
+            off = T["FU%d" % t][:, a // 16:b // 16]
+            do("v", lambda e: e.tensor_tensor(out=ap(o), in0=ap(rg("AX")).indirect(off), in1=T.U[:, a:b], op=OP.max),
+               [rg("AX"), rg("FU%d" % t), rg("U", a, b)], [o], 0.05 + (b - a) * GA * CY)
+        for j, (a, b) in enumerate(AH):
+            half(a, b)
+            ts(rg("WJ", a, b), rg("WI", a, b), 4095, OP.bitwise_and)
+            cp(rg("AS%d" % t, a, b), rg("WJ", a, b))
+            send("mA%d_%d" % (t, j))
+
+    def sites(t, out):
+        row = "VF"
+        if t < RO - 1:
+            ts(rg("VB"), rg("VW%d" % t), 0.0, OP.is_ge)
+            row = "VB"
+        rowlist(("RL", 256, 288), row, 0, 512)
+        ts(rg("VLB", 0, 32), ("RL", 256, 288), 0.0625, OP.mult)
+        cp(rg("VLB", 32, 64), rg("LS%d" % t, 32, 64))
+        ts(rg("XK"), rg("XI", 0, 1), 15, OP.bitwise_and)
+        cp(rg("XKF"), rg("XK"))
+        ts(rg("PM"), rg("M16B"), rg("XKF"), OP.is_equal)
+        ts(rg("XJ"), rg("XI"), 4, OP.arith_shift_right)
+        tt(rg("XM"), rg("XJ"), rg("DM"), OP.mult)
+
+        def half(j):
+            do("v", lambda e: e.tensor_reduce(T.HL[:, j:j + 1], T.XM[:, 16 * j:16 * j + 16], AxisListType.X, OP.add), [rg("XM")], [("HL", j, j + 1)], el(16))
+        half(0)
+        half(1)
+        cp(rg("HLU"), rg("HL", 0, 2))
+        gat(rg("GXL", 0, 32), rg("VLB", 0, 32), rg("HLU"))
+        gat(rg("GXL", 32, 64), rg("VLB", 32, 64), rg("HLU"))
+        do("p", mmf(("RL", 320, 384), rg("PM"), rg("GXL"), True, True), [rg("PM"), rg("GXL")], [("RL", 320, 384)], 64 * PE)
+        tt(rg("BO"), rg("VLB", 0, 32), ("RL", 320, 352), OP.mult)
+        tt(rg("BD"), ("RL", 352, 384), rg("VLB", 32, 64), OP.subtract)
+        if t == 0:
+            tt(out, rg("BO"), rg("BD"), OP.mult)
+        else:
+            tt(rg("BD"), rg("BO"), rg("BD"), OP.mult)
+            tt(out, rg("BD"), rg("VLB", 32, 64), OP.add)
+
+    def turns(t):
+        ts(rg("TL"), ("SLB", 16 * t, 16 * t + 16), 4.0, OP.is_le)
+        tt(rg("DFG"), rg("LS%d" % t, 16, 32), rg("LS%d" % t, 0, 16), OP.subtract)
+        if t == 0:
+            tt(rg("DL0", 0, 16), rg("TL"), rg("DFG"), OP.mult)
+            ts(rg("DL0", 16, 32), rg("DL0", 0, 16), -1.0, OP.mult)
+            return
+        tt(rg("TD"), rg("TL"), rg("DFG"), OP.mult)
+        if t < RO - 1:
+            tt(rg("LO%d" % t, 0, 16), rg("LS%d" % t, 0, 16), rg("TD"), OP.add)
+            tt(rg("LO%d" % t, 16, 32), rg("LS%d" % t, 16, 32), rg("TD"), OP.subtract)
+        else:
+            tt(rg("YF"), rg("LS%d" % t, 0, 16), rg("TD"), OP.add)
+            dma("y", T.yf[:], T.YF[:], "yf", [rg("YF")], [], 8192)
+            tt(rg("DAN"), rg("ALF"), rg("NLF"), OP.subtract)
+            tt(rg("TA"), rg("TL"), rg("DAN"), OP.mult)
+            tt(rg("YN"), rg("NLF"), rg("TA"), OP.add)
+            dma("y", T.yn[:], T.YN[:], "yn", [rg("YN")], [], 8192)
+
+    last = len(CH) - 1
+    start()
+    for t in range(RO):
+        for role in ("H", "A"):
+            for c, (a, b) in enumerate(CH):
+                frames(role, t, a, b)
+                maxima(role, a, b)
+                sums(role, c, a, b)
+        take(t)
+        take_lists(t)
+        if t == RO - 1:
+            boxes_of_sites()
+        for c in range(last):
+            decide(t, c)
+        if t < RO - 1:
+            store(t, 0, CH[last][0])
+        decide(t, last)
+        if t < RO - 1:
+            store(t, CH[last][0], P)
+        xor_list()
+        if t < RO - 1:
+            partners(t)
+            turns(t)
+            sites(t, rg("DL0" if t == 0 else "LO%d" % t, 32, 64))
+            send("mL%d" % t)
+        else:
+            dma("y", T.yc[:], T.YC[:], "yc", [rg("YC")], [], 262144)
+            sites(t, rg("YB"))
+            dma("s", T.yb[:], T.YB[:], "yb", [rg("YB")], [], 16384)
+            turns(t)
+    for o in arrange(ops):
+        issue(o)
+
+    for sem, val in list(cnt.items()) + list(total.items()):
+        wait("g", sem, val, {})
+    g.wait_ge(T.sem.loc, NE * len(MSGS))

@@ -2,10 +2,14 @@ from concourse.mybir import AluOpType as OP, AxisListType, ActivationFunctionTyp
 
 P, WX, RO = 256, 4096, 3
 CH = [(0, 64), (64, 128), (128, 192), (192, 256)]
-AH = [(0, 128), (128, 256)]
+HC = CH
+HM = CH
+AM = [(0, 64), (64, 256)]
 NE = 8
 FRAC = -0.5 + 2.0 ** -10
-CY, GA, SC, PE, WK, HOP = 0.00083, 1.56, 3.8, 0.00046, 0.15, 7.0
+SH = 25.0 / 64
+BIG = 1.5 * 2.0 ** 27
+CY, GA, SC, PE, WK, HOP = 0.00083, 1.56, 3.8, 0.00042, 0.16, 7.0
 
 SCRATCH = {}
 
@@ -14,55 +18,45 @@ def _sb(name, cols, dtype="float32"):
     SCRATCH[name] = ("sbuf", [128, cols], dtype)
 
 
-for _n, _c, _d in [
-        ("X", WX, "bfloat16"), ("CBI", 512, "int32"), ("BSI", 32, "int32"), ("FSI", 16, "int32"), ("NBI", 16, "int32"), ("THI", 1, "int32"),
-        ("PFB", 256, "bfloat16"), ("PNB", 256, "bfloat16"), ("LU0", 64, "uint16"), ("CS", 512, "int32"),
-        ("CF", 4096, "bfloat16"), ("CN", 4096, "bfloat16"), ("GH", 4096, "bfloat16"), ("GA", 4096, "bfloat16"),
-        ("OHF", 4096, "bfloat16"), ("OHN", 4096, "bfloat16"), ("OAF", 4096, "bfloat16"), ("OAN", 4096, "bfloat16"),
-        ("KHF", 256, "bfloat16"), ("KHN", 256, "bfloat16"), ("KAF", 256, "bfloat16"), ("KAN", 256, "bfloat16"),
-        ("SEL", 2064, "bfloat16"), ("NSEL", 2064, "bfloat16"), ("ONE", 128, "bfloat16"), ("BLK0", 128, "bfloat16"), ("BLK", 128, "bfloat16"),
-        ("IDN", 128, "bfloat16"), ("ONF", 128, "float32"), ("BLKF", 128, "float32"),
-        ("M16", 128, "float32"), ("MB0", 128, "float32"), ("M16B", 128, "float32"), ("IC16", 32, "float32"), ("VC", 32, "bfloat16"), ("VLO", 32, "bfloat16"),
-        ("IOV", 512, "float32"), ("DM", 32, "float32"),
-        ("LBI", 128, "int32"), ("LBJ", 128, "int32"), ("LP", 128, "bfloat16"), ("RBI", 32, "int32"), ("RBJ", 32, "int32"), ("RP", 32, "bfloat16"),
-        ("E15", 16, "float32"), ("INV", 512, "float32"), ("GROW", 256, "float16"), ("BROW", 512, "float32"), ("EF", 512, "float32"),
-        ("AROW", 256, "float16"), ("NROW", 256, "float16"), ("AL", 16, "uint16"), ("NL", 16, "uint16"), ("ALF", 16, "float32"), ("NLF", 16, "float32"),
-        ("SW", 256, "bfloat16"), ("RS", 8, "float32"), ("HN", 256, "float32"), ("AN", 256, "float32"), ("AM", 256, "float32"), ("V", 256, "float32"), ("U", 256, "float32"),
-        ("LH", 128, "bfloat16"), ("XL", 32, "uint16"), ("XI", 32, "int32"), ("XJ", 32, "int32"),
-        ("PM", 128, "bfloat16"), ("XM", 32, "float32"), ("HL", 8, "float32"), ("HLU", 2, "uint16"),
-        ("AX", 512, "float32"), ("WI", 256, "int32"), ("WJ", 256, "int32"), ("VB", 512, "bfloat16"), ("VLB", 64, "float32"), ("GXL", 64, "float16"),
-        ("BO", 32, "float32"), ("BD", 32, "float32"), ("TL", 16, "float32"), ("DFG", 16, "float32"), ("TD", 16, "float32"), ("DAN", 16, "float32"), ("TA", 16, "float32"),
-        ("XC", 16, "uint16"), ("XDF", 256, "float32"), ("FLG", 256, "bfloat16"),
-        ("YC", 512, "float32"), ("YB", 32, "float32"), ("YF", 16, "float32"), ("YN", 16, "float32"),
-        ("VW0", 512, "float32"), ("VW1", 512, "float32"), ("VF", 512, "bfloat16"), ("DL0", 64, "float32"), ("DR0", 64, "float32"), ("LE0", 64, "float32"),
-        ("AF", 256, "float32"), ("HF", 256, "float32"), ("DD", 256, "float32"), ("AMF", 256, "float32")]:
-    _sb(_n, _c, _d)
+for _d, _l in (
+        ("bfloat16", "X:4096 PFB:256 PNB:256 CF:4096 CN:4096 GH:4096 GA:4096 OHF:4096 OHN:4096 OAF:4096 OAN:4096 KHF:256 KHN:256 KAF:256 KAN:256 "
+                     "SEL:144 NSEL:144 SEL16:144 ONE:128 BLK0:128 BLK:128 IDN:128 BR:128 K1024:128 WB0:128 WB:128 BITS:640 RP0:16 RP1:16 RP2:16 J4:16 "
+                     "ILB:16 EB:16 SW:256 FB:256 RH:256 LOW:16 LH:128 PM:128 VB:512 VF:512 FLG:256"),
+        ("int32", "CBI:512 BSI:32 FSI:16 NBI:16 THI:1 CS:512 BI:640 BJ:640 WI:256 WJ:256"),
+        ("uint16", "LU0:64 FG:32 AL:32 XC:16 EU:16 HLU:4"),
+        ("float16", "GROW:256 FH:16 EF:512 NROW:512 GXL:64"),
+        ("float32", "M16:128 MB0:128 M16B:128 NCM:128 D0:128 D1:128 WR:128 IOV:640 IC16:16 INV:512 BROW:512 LA:32 LB:32 "
+                    "HF:256 AF:256 DD:256 HN:256 AN:256 QS:256 XDF:256 YC:512 YB:32 YF:16 YN:16 VW0:528 VW1:528")):
+    for _e in _l.split():
+        _sb(_e.split(":")[0], int(_e.split(":")[1]), _d)
 for _t in range(RO):
-    for _n, _c, _d in [("AU", 256, "uint16"), ("HU", 256, "uint16"), ("LS", 64, "float32"), ("FU", 32, "uint16")]:
+    for _n, _c, _d in [("AU", 256, "uint16"), ("HU", 256, "uint16"), ("LS", 96, "float32"), ("FU", 16, "uint16")]:
         _sb(_n + str(_t), _c, _d)
     if _t < RO - 1:
         for _n, _c, _d in [("AS", 256, "uint16"), ("HS", 256, "uint16"), ("LO", 64, "float32")]:
             _sb(_n + str(_t), _c, _d)
 ALIAS = {}
-for _k, _d, _l in (("KF", "float32", [(n, 1) for n in "PL PL16 PW PWS ADS P2 NP2 TH2 HBF XKF".split()]),
-                   ("KI", "int32", [(n, 16) for n in "EI EJ UI UJ UK IL16".split()] + [(n, 1) for n in "PI PJ HBI HBJ XK".split()])):
+for _k, _d, _l in (("KF", "float32", "PL:1 PWH:1 PW:1 PR:1 P9:1 P2:1 NP2:1 CC:1 TH2:1 TS:1 HB:1 DM:16 DW:16 IL:16 E16:16 LB0:16 LIM:16 LT:16 LF:16 "
+                                     "MW:16 XW:16 TL:16 DFG:16 TD:16 DAN:16 TA:16 BO:32 BD:32 BE:32"),
+                   ("KI", "int32", "EI:16 EJ:16 PI:1 PJ:1 RI:1")):
     _o = 0
-    for _n, _w in _l:
-        ALIAS[_n] = (_k, _o, _w)
-        _o += _w
+    for _e in _l.split():
+        ALIAS[_e.split(":")[0]] = (_k, _o, int(_e.split(":")[1]))
+        _o += int(_e.split(":")[1])
     _sb(_k, _o, _d)
 PS = ["Z0", "Z1", "Z2", "Z3", "VT", "PF", "SLB", "RL"]
 for _n in PS:
     SCRATCH[_n] = ("psum", [128, 512], "float32")
 
-MSGS = [("mE", "LS0", "LE0", 0, 64)]
+MSGS = []
 for _t in range(RO - 1):
-    MSGS += [("mH%d_%d" % (_t, _c), "HS%d" % _t, "HU%d" % (_t + 1), _a, _b) for _c, (_a, _b) in enumerate(CH)]
-    MSGS += [("mA%d_%d" % (_t, _c), "AS%d" % _t, "AU%d" % (_t + 1), _a, _b) for _c, (_a, _b) in enumerate(AH)]
-    MSGS += [("mL%d" % _t, "DL0" if _t == 0 else "LO%d" % _t, "DR0" if _t == 0 else "LS%d" % (_t + 1), 0, 64)]
-LOADS = ["NBI", "CBI", "BSI", "FSI", "THI", "PFB", "PNB", "X"]
+    MSGS += [("mH%d_%d" % (_t, _c), "HS%d" % _t, "HU%d" % (_t + 1), _a, _b) for _c, (_a, _b) in enumerate(HM)]
+    MSGS += [("mA%d_%d" % (_t, _c), "AS%d" % _t, "AU%d" % (_t + 1), _a, _b) for _c, (_a, _b) in enumerate(AM)]
+    MSGS += [("mL%d" % _t, "LO%d" % _t, "LS%d" % (_t + 1), 0, 64)]
+MSGS += [("mB", "LA", "LB", 0, 32)]
+LOADS = [("y", "NBI", "nb"), ("s", "PFB", "pf"), ("y", "BSI", "bs"), ("s", "PNB", "pn"), ("y", "CBI", "cb"), ("s", "FSI", "fs"), ("y", "X", "xf"), ("s", "THI", "th")]
 OUTS = ["yc", "yb", "yf", "yn"]
-SEMAPHORES = ["sv", "ss", "sp", "sg", "loc"] + [m[0] for m in MSGS] + ["d" + n for n in LOADS + OUTS]
+SEMAPHORES = ["sv", "ss", "sp", "sg", "loc"] + [m[0] for m in MSGS] + ["d" + n[1] for n in LOADS] + ["d" + n for n in OUTS]
 
 
 def hop(core, dst, topo, T):
@@ -114,34 +108,27 @@ def arrange(ops):
     for i in range(n):
         for j in pred[i]:
             succ[j].append(i)
+
+    def lag(i, j):
+        return 0.0 if ops[i]["q"] == "p" and ops[j]["q"] == "p" else WK
     rank = [0.0] * n
     for i in range(n - 1, -1, -1):
-        rank[i] = ops[i]["cost"] + max([rank[j] + WK for j in succ[i]] + [0.0])
-    left = [len(p) for p in pred]
-    ready = [0.0] * n
-    free = {}
-    avail = [i for i in range(n) if left[i] == 0]
-    order = []
-    while avail:
-        best = None
-        for i in avail:
-            o = ops[i]
-            st = max(free.get(o["q"], 0.0), ready[i]) if o["q"] != "r" else ready[i]
-            key = (st - (0.02 * min(rank[i], 60.0)), -rank[i], i)
-            if best is None or key < best[0]:
-                best = (key, i, st)
-        _, i, st = best
-        avail.remove(i)
-        end = st + ops[i]["cost"]
-        if ops[i]["q"] != "r":
-            free[ops[i]["q"]] = st + ops[i]["hold"]
-        order.append((st, len(order), i))
-        for j in succ[i]:
-            left[j] -= 1
-            ready[j] = max(ready[j], end + WK)
-            if left[j] == 0:
-                avail.append(j)
-    return [ops[i] for _, _, i in order]
+        rank[i] = ops[i]["cost"] + max([rank[j] + lag(i, j) for j in succ[i]] + [0.0])
+    start = [0.0] * n
+    taken = {}
+    for i in sorted(range(n), key=lambda i: (-rank[i], i)):
+        st = max([start[j] + ops[j]["cost"] + lag(j, i) for j in pred[i]] + [0.0])
+        hold = ops[i]["hold"]
+        if hold:
+            line = taken.setdefault(ops[i]["q"], [])
+            for lo, hi in line:
+                if st + hold <= lo:
+                    break
+                st = max(st, hi)
+            line.append((st, st + hold))
+            line.sort()
+        start[i] = st
+    return [ops[i] for i in sorted(range(n), key=lambda i: (start[i], i))]
 
 
 def rank_program(g, core, T, topo):
@@ -159,7 +146,7 @@ def rank_program(g, core, T, topo):
     acc = {}
     total = {}
     ops = []
-    index = {}
+    read = []
 
     def wait(q, sem, val, know):
         k = known[q]
@@ -205,16 +192,16 @@ def rank_program(g, core, T, topo):
         ops.append({"kind": kind, "q": q, "fns": fns, "rd": rd, "wr": wr, "cost": cost, "hold": cost if hold is None else hold, "after": after, "extra": extra})
         return len(ops) - 1
 
-    def do(q, fns, rd, wr, cost):
-        return add("do", q, fns if isinstance(fns, list) else [fns], rd, wr, cost)
+    def do(q, fns, rd, wr, cost, after=()):
+        return add("do", q, fns if isinstance(fns, list) else [fns], rd, wr, cost, None, after)
 
-    def dma(q, out, in_, name, rd, wr, size):
-        add("dma", q, [lambda e: e.dma_start(out=out, in_=in_)], rd, wr, 2.0 + size / 220e3, 0.1, (), "d" + name)
+    def dma(q, out, in_, name, rd, wr, cost):
+        add("dma", q, [lambda e: e.dma_start(out=out, in_=in_)], rd, wr, cost, 0.1, (), "d" + name)
 
     def send(sem):
         _, src, land, a, b = [m for m in MSGS if m[0] == sem][0]
         i = add("send", "g", None, [(src, a, b)], [("SENDQ", 0, 1)], 1.0, 1.0, (), sem)
-        add("land", "r", None, [], [(land, a, b)], HOP, 0.0, (i,), sem)
+        add("land", "r", None, [], [(land, a, b)], HOP - 1.0, 0.0, (i,), sem)
 
     def issue(o):
         q = o["q"]
@@ -248,6 +235,9 @@ def rank_program(g, core, T, topo):
     def ap(x):
         return T[x[0]][:, x[1]:x[2]]
 
+    def val(s):
+        return ap(s) if isinstance(s, tuple) else s
+
     def two(x):
         return SCRATCH[x[0]][0] == "sbuf" and SCRATCH[x[0]][2] in ("bfloat16", "float16", "uint16")
 
@@ -256,44 +246,58 @@ def rank_program(g, core, T, topo):
 
     def tt(o, x, y, op):
         f = 1.0 if x[0] in PS or y[0] in PS else 2.0
-        do("v", lambda e: e.tensor_tensor(out=ap(o), in0=ap(x), in1=ap(y), op=op), [x, y], [o], el(o[2] - o[1], f))
+        return do("v", lambda e: e.tensor_tensor(out=ap(o), in0=ap(x), in1=ap(y), op=op), [x, y], [o], el(o[2] - o[1], f))
 
     def ts(o, x, s1, op0, s2=None, op1=None):
         rd = [x] + [s for s in (s1, s2) if isinstance(s, tuple)]
-        a1 = ap(s1) if isinstance(s1, tuple) else s1
-        a2 = ap(s2) if isinstance(s2, tuple) else s2
         c = el(o[2] - o[1], 0.5 if two(o) and two(x) else 1.0)
         if op1 is None:
-            do("v", lambda e: e.tensor_scalar(out=ap(o), in0=ap(x), scalar1=a1, scalar2=None, op0=op0), rd, [o], c)
-        else:
-            do("v", lambda e: e.tensor_scalar(out=ap(o), in0=ap(x), scalar1=a1, scalar2=a2, op0=op0, op1=op1), rd, [o], c)
+            return do("v", lambda e: e.tensor_scalar(out=ap(o), in0=ap(x), scalar1=val(s1), scalar2=None, op0=op0), rd, [o], c)
+        return do("v", lambda e: e.tensor_scalar(out=ap(o), in0=ap(x), scalar1=val(s1), scalar2=val(s2), op0=op0, op1=op1), rd, [o], c)
 
-    def cp(o, x, out=None, in_=None):
+    def cp(o, x, out=None, in_=None, n=None):
         w, r = out if out is not None else ap(o), in_ if in_ is not None else ap(x)
-        do("v", lambda e: e.tensor_copy(out=w, in_=r), [x], [o], el(max(x[2] - x[1], o[2] - o[1]) if out is None else 256, 0.5 if two(o) and two(x) else 1.0))
+        do("v", lambda e: e.tensor_copy(out=w, in_=r), [x], [o], el(n or x[2] - x[1], 0.5 if two(o) and two(x) else 1.0))
 
-    def act(out, in_, rd, wr, n, scale=1.0):
-        do("s", lambda e: e.activation(out, in_, AF.Copy, scale=scale), rd, wr, n * CY + 0.05)
+    def act(o, x, func=AF.Copy, scale=1.0, bias=None, out=None, n=None, after=()):
+        w = out if out is not None else ap(o)
+        c = max(64, n or x[2] - x[1]) * CY + 0.05
+        if bias is None:
+            return do("s", lambda e: e.activation(w, ap(x), func, scale=scale), [x], [o], c, after)
+        return do("s", lambda e: e.activation(w, ap(x), func, bias=bias, scale=scale), [x], [o], c, after)
+
+    def red(o, x):
+        do("v", lambda e: e.tensor_reduce(ap(o), ap(x), AxisListType.X, OP.add), [x], [o], el(x[2] - x[1]))
 
     def fill(o, c):
         do("v", lambda e: e.memset(ap(o), c), [], [o], el(o[2] - o[1], 0.5 if two(o) else 1.0))
 
-    def gat(o, win, off):
-        do("v", lambda e: e.tensor_copy(out=ap(o), in_=ap(win).indirect(ap(off))), [win, off], [o], 0.05 + (o[2] - o[1]) * GA * CY)
+    def gat(o, win, off, q="v", after=()):
+        c = 0.06 + (o[2] - o[1]) * GA * CY
+        if q == "v":
+            do("v", lambda e: e.tensor_copy(out=ap(o), in_=ap(win).indirect(ap(off))), [win, off], [o], c)
+        else:
+            return do("s", lambda e: e.activation(ap(o), ap(win).indirect(ap(off)), AF.Copy), [win, off], [o], c, after)
 
-    def sca(win, off, x):
-        do("v", lambda e: e.tensor_copy(out=ap(win).indirect(ap(off)), in_=ap(x)), [x, off], [win], 0.05 + (x[2] - x[1]) * SC * CY)
+    def sca(win, off, x, y=None, op=None):
+        c = 0.05 + (x[2] - x[1]) * SC * CY
+        if y is None:
+            do("v", lambda e: e.tensor_copy(out=ap(win).indirect(ap(off)), in_=ap(x)), [x, off], [win], c)
+        else:
+            do("v", lambda e: e.tensor_tensor(out=ap(win).indirect(ap(off)), in0=ap(x), in1=ap(y), op=op), [x, y, off], [win], c)
 
-    def mmf(o, l, r, start, stop, kp=128):
-        return lambda e: e.matmul(ap(o), T[l[0]][0:kp, l[1]:l[2]], T[r[0]][0:kp, r[1]:r[2]], start, stop)
+    def mm(o, terms, after=(), whole=False):
+        fl, rd = [], []
+        for l, r, kp in terms:
+            rd += [l, r]
+            if kp is None:
+                fl += [(T[l[0]][:, 15 - k:143 - k], T[r[0]][:, r[1] + k:r[2]:16]) for k in range(16)]
+            else:
+                fl.append((T[l[0]][0:kp, l[1]:l[2]], T[r[0]][0:kp, r[1]:r[2]]))
 
-    def sel(neg, k):
-        return T["NSEL" if neg else "SEL"][:, 128 * k:128 * k + 128]
-
-    def rowlist(o, row, a, b):
-        def one(l):
-            return lambda e: e.matmul(ap(o), sel(0, l), T[row][:, a + l:b:16], l == 0, l == 15)
-        do("p", [one(l) for l in range(16)], [rg("SEL"), (row, a, b)], [o], 1024 * PE)
+        def one(i):
+            return lambda e: e.matmul(ap(o), fl[i][0], fl[i][1], i == 0, i == len(fl) - 1)
+        return do("p", [one(i) for i in range(len(fl))], rd, [o], len(fl) * max(64, o[2] - o[1]) * PE, after)
 
     def aff(o, x, pat, op, fillv, base, cm):
         do("g", lambda e: e.affine_select(ap(o), ap(x), pat, op, fillv, base, cm), [x], [o], 0.17 + 2 * (o[2] - o[1]) * CY)
@@ -303,76 +307,86 @@ def rank_program(g, core, T, topo):
            [], [o], 0.13 + 2 * (o[2] - o[1]) * CY)
 
     def start():
-        for q, n, src in (("y", "NBI", "nb"), ("y", "CBI", "cb"), ("s", "PFB", "pf"), ("s", "PNB", "pn"), ("y", "BSI", "bs"), ("y", "FSI", "fs"), ("y", "X", "xf"), ("s", "THI", "th")):
-            dma(q, T[n][:], T[src][:], n, [], [rg(n)], 128 * SCRATCH[n][1][1] * 3)
-        for n, c in (("ONE", 1.0), ("PW", 1.0), ("ADS", FRAC), ("SEL", 0.0), ("NSEL", 0.0)):
+        size = 0
+        for q, n, src in LOADS:
+            size += 128 * SCRATCH[n][1][1] * (2 if two(rg(n)) else 4)
+            dma(q, T[n][:], T[src][:], n, [], [rg(n)], 2.2 + size / 220e3)
+        for n, c in (("ONE", 1.0), ("SEL", 0.0), ("VW0", -16384.0), ("VW1", -16384.0), ("VF", -1.0)):
             fill(rg(n), c)
         aff(rg("BLK0"), rg("ONE"), [[-16, 8], [0, 16]], OP.is_ge, 0.0, 0, 1)
         aff(rg("BLK"), rg("BLK0"), [[16, 8], [0, 16]], OP.is_ge, 0.0, 15, -1)
-        iota(rg("PI"), [[0, 1]], 0, 1, False)
-        iota(rg("M16"), [[0, 8], [1, 16]], 0, 0)
-        for m in range(8):
-            s0 = 16 * m
-            cp(("SEL", m, m + 1), rg("BLK"), T.SEL[:, s0:s0 + 129 * 15 + 1:129], T.BLK[:, s0:s0 + 16])
-            act(T.NSEL[:, s0:s0 + 129 * 15 + 1:129], T.BLK[:, s0:s0 + 16], [rg("BLK")], [("NSEL", m, m + 1)], 16, -1.0)
+        aff(rg("IDN"), rg("ONE"), [[-1, 128]], OP.is_equal, 0.0, 0, 1)
+        cp(rg("SEL"), rg("BLK"), T.SEL[:, 15:143:16], T.BLK[:, 0:128:16], 8)
+        ts(rg("NSEL"), rg("SEL"), -1.0, OP.mult)
+        ts(rg("SEL16"), rg("SEL"), 0.0625, OP.mult)
+        ts(rg("K1024"), rg("IDN"), 16.0, OP.mult)
+        tt(rg("BR"), rg("K1024"), rg("BLK"), OP.add)
+        ts(rg("K1024"), rg("IDN"), 1024.0, OP.mult)
         cp(rg("LU0", 48, 64), rg("NBI"))
         gat(rg("HU0"), rg("CBI"), rg("LU0", 48, 64))
         cp(rg("LU0", 0, 32), rg("BSI"))
         gat(rg("CS"), rg("CBI"), rg("LU0", 0, 32))
-        cp(rg("LU0", 32, 48), rg("FSI"))
-        gat(rg("AU0"), rg("CS"), rg("LU0", 32, 48))
+        cp(rg("FU0"), rg("FSI"))
+        gat(rg("AU0"), rg("CS"), rg("FU0"))
         for k in range(16):
             cp(("CF", k, k + 1), rg("PFB"), T.CF[:, k:4096:16], T.PFB[:, :])
-            if k < 8:
-                act(T.CN[:, k:4096:16], T.PNB[:, :], [rg("PNB")], [("CN", k, k + 1)], 256)
-            else:
-                cp(("CN", k, k + 1), rg("PNB"), T.CN[:, k:4096:16], T.PNB[:, :])
-        cp(rg("PF", 0, 256), rg("PFB"))
-        cp(rg("PF", 256, 512), rg("PNB"))
-        aff(rg("IDN"), rg("ONE"), [[-1, 128]], OP.is_equal, 0.0, 0, 1)
-        iota(rg("IC16"), [[16, 32]], 0, 0)
-        iota(rg("IOV"), [[1, 512]], 0, 0)
-        aff(rg("MB0"), rg("M16"), [[-16, 8], [0, 16]], OP.is_ge, 99.0, 0, 1)
-        aff(rg("M16B"), rg("MB0"), [[16, 8], [0, 16]], OP.is_ge, 99.0, 15, -1)
-        for b in range(1, 9):
-            aff(rg("PW"), rg("PW"), [[0, 1]], OP.not_equal, 2.0 ** -b, -b, 1)
-        aff(rg("PWS"), rg("PW"), [[0, 1]], OP.not_equal, 0.0, 0, 1)
-        aff(rg("ADS"), rg("ADS"), [[0, 1]], OP.not_equal, 1.0, 0, 1)
-        fill(rg("ONF"), 1.0)
+            act(("CN", k, k + 1), rg("PNB"), out=T.CN[:, k:4096:16])
+        act(rg("PF", 0, 256), rg("PFB"))
+        act(rg("PF", 256, 512), rg("PNB"))
+        iota(rg("PI"), [[0, 1]], 0, 1, False)
+        iota(rg("M16"), [[0, 8], [1, 16]], 0, 0)
+        iota(rg("IC16"), [[16, 16]], 0, 0)
+        iota(rg("IOV", 0, 512), [[1, 512]], 0, 0)
+        iota(rg("IOV", 512, 640), [[0, 8], [17, 16]], 0, 0)
         ts(rg("PJ"), rg("PI"), 15, OP.bitwise_and)
         cp(rg("PL"), rg("PJ"))
-        ts(rg("PL16"), rg("PL"), 16.0, OP.mult)
-        ts(rg("TH2"), rg("THI"), 0.5, OP.mult)
-        ts(rg("DM"), rg("M16", 0, 32), rg("PL"), OP.is_equal)
-        ts(rg("VLO"), rg("ONE", 0, 32), rg("PL"), OP.mult)
-        cp(rg("VC"), rg("IC16"))
-        ts(rg("IL16"), rg("IC16", 0, 16), 16.0, OP.mult, rg("PL16"), OP.add)
-        do("v", lambda e: e.reciprocal(ap(rg("P2")), ap(rg("PW"))), [rg("PW")], [rg("P2")], 0.2)
+        ts(rg("DM"), rg("M16", 0, 16), rg("PL"), OP.is_equal)
+        ts(rg("D0"), rg("M16"), 0.0, OP.not_equal, 0.5, OP.mult)
+        ts(rg("D1"), rg("M16"), 0.0, OP.is_equal, 0.5, OP.mult)
+        do("v", lambda e: e.tensor_tensor_scan(T.WR[:, :], T.D0[:, :], T.D1[:, :], 0.0, OP.mult, OP.add), [rg("D0"), rg("D1")], [rg("WR")], el(128))
+        cp(rg("WB"), rg("WR"))
+        aff(rg("WB0"), rg("WB"), [[0, 8], [1, 16]], OP.is_ge, 0.0, -1, 0)
+        aff(rg("WB"), rg("WB0"), [[0, 8], [-1, 16]], OP.is_ge, 0.0, 8, 0)
+        tt(rg("DW"), rg("WR", 0, 16), rg("DM"), OP.mult)
+        red(rg("PWH"), rg("DW"))
+        ts(rg("PW"), rg("PWH"), 2.0, OP.mult)
+        do("v", lambda e: e.reciprocal(ap(rg("PR")), ap(rg("PW"))), [rg("PW")], [rg("PR")], 0.2)
+        ts(rg("P9"), rg("PL"), 9.0, OP.is_lt)
+        tt(rg("P2"), rg("PR"), rg("P9"), OP.mult)
         ts(rg("NP2"), rg("P2"), -2.0, OP.mult)
-        for bi, bj, src, o, n in (("LBI", "LBJ", "M16", "LP", 128), ("RBI", "RBJ", "IC16", "RP", 32)):
-            ts(rg(bi), rg(src, 0, n), rg("PW"), OP.mult, FRAC, OP.add)
-            ts(rg(bj), rg(bi), 1, OP.bitwise_and)
-            ts(rg(o), rg(bj), rg("NP2"), OP.mult, rg("P2"), OP.add)
-        cp(rg("BLKF"), rg("BLK"))
-        rowlist(rg("RL", 0, 16), "PFB", 0, 256)
+        ts(rg("CC"), rg("PL"), 1.0, OP.min, -0.5, OP.mult)
+        ts(rg("BI"), rg("IOV"), rg("PW"), OP.mult, FRAC, OP.add)
+        ts(rg("BJ"), rg("BI"), 1, OP.bitwise_and)
+        ts(rg("BITS"), rg("BJ"), rg("NP2"), OP.mult, rg("P2"), OP.add)
+        ts(rg("TH2"), rg("THI"), 0.5, OP.mult)
+        aff(rg("MB0"), rg("M16"), [[-16, 8], [0, 16]], OP.is_ge, 99.0, 0, 1)
+        aff(rg("M16B"), rg("MB0"), [[16, 8], [0, 16]], OP.is_ge, 99.0, 15, -1)
+        ts(rg("NCM"), rg("M16B"), -1.0, OP.mult, rg("PL"), OP.add)
+        iota(rg("RP0", 0, 4), [[0, 2], [-2, 2]], 1, 0)
+        aff(rg("RP1", 0, 4), rg("RP0", 0, 4), [[0, 4]], OP.is_equal, 1.0, -8, 1)
+        aff(rg("RP0", 0, 4), rg("RP1", 0, 4), [[0, 4]], OP.is_ge, 0.0, -4, 1)
+        ts(rg("RP2", 0, 4), rg("RP0", 0, 4), 0.0625, OP.mult)
+        ts(rg("J4", 0, 4), rg("IC16", 0, 4), rg("PL"), OP.add)
+        ts(rg("IL"), rg("IC16"), rg("PL"), OP.add)
+        cp(rg("ILB"), rg("IL"))
+        mm(rg("RL", 0, 16), [(rg("SEL"), rg("PFB"), None)])
         cp(rg("EI"), rg("RL", 0, 16))
         ts(rg("EJ"), rg("EI"), 15, OP.bitwise_and)
-        cp(rg("E15"), rg("EJ"))
-        fill(rg("VW0"), -16384.0)
-        fill(rg("VW1"), -16384.0)
-        fill(rg("VF"), 0.0)
+        ts(rg("E16"), rg("EJ"), 0.0625, OP.mult)
+        ts(rg("EB"), rg("E16"), SH, OP.add)
+        tt(rg("LB0"), rg("IL"), rg("E16"), OP.add)
+        ts(rg("LIM"), rg("IL"), 1.0, OP.add)
+        ts(rg("LT"), rg("LB0"), 4.5 / 16, OP.add)
+        ts(rg("LF"), rg("LB0"), 8.5 / 16, OP.add)
         cp(rg("LS0", 0, 16), rg("FSI"))
         cp(rg("LS0", 32, 64), rg("BSI"))
-        sca(rg("INV"), rg("LU0", 0, 32), rg("IOV"))
+        sca(rg("INV"), rg("LU0", 0, 32), rg("IOV", 0, 512))
         gat(rg("GROW"), rg("INV"), rg("LU0", 48, 64))
-        rowlist(rg("RL", 16, 32), "GROW", 0, 256)
-        ts(rg("LS0", 16, 32), rg("RL", 16, 32), 0.0625, OP.mult)
-        send("mE")
+        mm(rg("RL", 16, 32), [(rg("SEL16"), rg("GROW"), None)])
+        cp(rg("LS0", 16, 32), rg("RL", 16, 32))
 
     def frames(role, t, a, b):
-        u = T[role + "U%d" % t][:, a:b]
-        o = ("G" + role, 16 * a, 16 * b)
-        do("s", lambda e: e.activation(ap(o), ap(rg("X")).indirect(u), AF.Copy), [rg("X"), rg(role + "U%d" % t, a, b)], [o], 0.065 + 16 * (b - a) * GA * CY)
+        read[:] = [gat(("G" + role, 16 * a, 16 * b), rg("X"), rg(role + "U%d" % t, a, b), "s", tuple(read))]
 
     def maxima(role, a, b):
         gx = ("G" + role, 16 * a, 16 * b)
@@ -382,14 +396,16 @@ def rank_program(g, core, T, topo):
             k = ("K" + role + f, a, b)
             do("v", lambda e: e.tensor_tensor(out=ap(k), in0=row0, in1=T.PF[:, o + a:o + b], op=OP.max), [gx, ("PF", o + a, o + b)], [k], el(b - a))
 
-        def rest(f, c):
-            o, d = ("O" + role + f, 16 * a, 16 * b), (c, 16 * a, 16 * b)
-            do("v", lambda e: e.tensor_tensor_scan(ap(o), ap(d), ap(gx), 255.0, OP.min, OP.max), [gx, rg(c)], [o], el(16 * (b - a), 0.5))
+        def rest(f, c, lo, hi):
+            o, d, x = ("O" + role + f, lo, hi), (c, lo, hi), (gx[0], lo, hi)
+            do("v", lambda e: e.tensor_tensor_scan(ap(o), ap(d), ap(x), 255.0, OP.min, OP.max), [x, rg(c)], [o], el(hi - lo, 0.5))
         first("F", 0)
         first("N", 256)
-        do("v", lambda e: e.memset(row0, 255.0), [], [gx], el(b - a))
-        rest("F", "CF")
-        rest("N", "CN")
+        do("v", lambda e: e.memset(row0, 255.0), [], [gx], el(b - a, 0.5))
+        for lo, hi in CH:
+            if a <= lo < b:
+                rest("F", "CF", 16 * lo, 16 * hi)
+                rest("N", "CN", 16 * lo, 16 * hi)
 
     def sums(role, c, a, b):
         z = ("Z%d" % c, 0, b - a)
@@ -397,187 +413,184 @@ def rank_program(g, core, T, topo):
         def one(f, k):
             neg = (role == "H") == (f == "F")
             rhs = T["O" + role + f][:, 16 * a + k:16 * b:16] if k else T["K" + role + f][:, a:b]
-            return lambda e: e.matmul(ap(z), sel(neg, k), rhs, role == "H" and f == "F" and k == 0, role == "A" and f == "N" and k == 15)
+            return lambda e: e.matmul(ap(z), T["NSEL" if neg else "SEL"][:, 15 - k:143 - k], rhs, role == "H" and f == "F" and k == 0, role == "A" and f == "N" and k == 15)
         for f in ("F", "N"):
-            neg = (role == "H") == (f == "F")
-            do("p", [one(f, k) for k in range(16)], [rg("NSEL" if neg else "SEL"), ("O" + role + f, 16 * a, 16 * b), ("K" + role + f, a, b)],
+            do("p", [one(f, k) for k in range(16)], [rg("NSEL"), rg("SEL"), ("O" + role + f, 16 * a, 16 * b), ("K" + role + f, a, b)],
                [(z[0], 0, 512) if (role, f) == ("H", "F") else z], 16 * max(64, b - a) * PE)
 
-    def boxes_of_sites():
-        for l in range(16):
-            act(T.EF[:, l:512:16], T.LS2[:, 32:64], [rg("LS2", 32, 64), rg("DM")], [("EF", l, l + 1)], 32, T.DM[:, l:l + 1])
-        do("p", mmf(rg("RL", 0, 512), rg("BLKF"), rg("EF"), True, True), [rg("BLKF"), rg("EF")], [rg("RL", 0, 512)], 2048 * PE)
-        act(ap(rg("BROW")), ap(rg("RL", 0, 512)), [rg("RL")], [rg("BROW")], 512)
-        for off, row, u, f in ((0, "AROW", "AL", "ALF"), (16, "NROW", "NL", "NLF")):
-            gat(rg(row), rg("BROW"), rg("FU2", off, off + 16))
-            rowlist(rg("RL", off, off + 16), row, 0, 256)
-            ts(rg(f), rg("RL", off, off + 16), 0.0625, OP.mult)
-            cp(rg(u), rg(f))
+    def boxes():
+        lo = "LO%d" % (RO - 2)
 
-    def take(t):
+        def spread(l):
+            do("v", lambda e: e.tensor_scalar(out=T.EF[:, l:512:16], in0=T[lo][:, 32:64], scalar1=ap(rg("DM", l, l + 1)), scalar2=None, op0=OP.mult),
+               [rg(lo, 32, 64), rg("DM")], [("EF", l, l + 1)], el(32))
+        for l in range(16):
+            spread(l)
+        mm(rg("RL"), [(rg("BLK"), rg("EF"), 128)])
+        act(rg("BROW"), rg("RL"))
+        cp(rg("FG"), rg(lo, 0, 32))
+        gat(rg("NROW"), rg("BROW"), rg("FG"))
+        mm(rg("RL", 0, 32), [(rg("SEL16"), rg("NROW"), None)])
+        cp(rg("LA"), rg("RL", 0, 32))
+        send("mB")
+
+    def take_nurses(t):
         cp(rg("HF"), rg("HU%d" % t))
-        cp(rg("AF"), rg("AU%d" % t))
-        tt(rg("DD"), rg("HF"), rg("AF"), OP.subtract)
-        if t < RO - 1:
-            ts(rg("AMF"), rg("AF"), -4096.0, OP.add)
+        cp(rg("VT", 256, 512), rg("HU%d" % t))
+
+    def take_flyers(t, a, b):
+        cp(rg("AF", a, b), rg("AU%d" % t, a, b))
+        tt(rg("DD", a, b) if t < RO - 1 else rg("VT", a, b), rg("VT", 256 + a, 256 + b), rg("AF", a, b), OP.subtract)
 
     def take_lists(t):
-        if t == 1:
-            tt(rg("LS1"), rg("LE0"), rg("DR0"), OP.add)
-        cp(rg("FU%d" % t), rg("LS%d" % t, 0, 32))
+        if t:
+            cp(rg("FU%d" % t), rg("LS%d" % t, 0, 16))
+        tt(rg("DFG"), rg("LS%d" % t, 16, 32), rg("LS%d" % t, 0, 16), OP.subtract)
+        if t < RO - 1:
+            cp(rg("FH"), rg("LS%d" % t, 0, 16))
+            gat(rg("FB"), rg("BITS", 0, 512), rg("FU%d" % t), "s")
+        else:
+            cp(rg("AL"), rg("LB"))
+            tt(rg("DAN"), rg("LB", 0, 16), rg("LB", 16, 32), OP.subtract)
 
     def decide(t, c):
         a, b = CH[c]
         n = b - a
-        z, sr = ("Z%d" % c, 0, n), ("Z%d" % c, 256, 256 + n)
+        z, r, sr = [("Z%d" % c, o, o + n) for o in (0, 128, 256)]
         sw = rg("SW", a, b)
         f = rg("FU%d" % t, a // 16, b // 16)
-        ts(sw, z, rg("TH2"), OP.is_gt)
-        do("p", mmf(sr, rg("BLK"), sw, True, True), [rg("BLK"), sw], [sr], 64 * PE)
-        rowlist(("SLB", 16 * t + a // 16, 16 * t + b // 16), "SW", a, b)
-        do("v", lambda e: e.tensor_reduce(T.RS[:, c:c + 1], ap(sw), AxisListType.X, OP.add), [sw], [("RS", c, c + 1)], el(n))
         if t < RO - 1:
+            ts(sw, z, rg("TH2"), OP.is_gt, -SH, OP.add)
+            mm(r, [(rg("BR"), sw, 128)])
+            mm(sr, [(rg("BLK"), sw, 128)])
             o = 128 * (c % 2)
-            tu, xs, xd, y = [("VT", o + 256 * (i // 2) + 64 * (i % 2), o + 256 * (i // 2) + 64 * (i % 2) + n) for i in range(4)]
-            ts(tu, sr, 4.0, OP.is_le)
-            tt(xs, tu, sw, OP.not_equal)
+            xs, xd = ("VT", o, o + n), ("VT", o + 64, o + 64 + n)
+            i = ts(xs, r, BIG, OP.add, BIG, OP.not_equal)
+            act(rg("QS", a, b), sr, AF.Identity, 8192.0, 8192.0 * (16 * SH - 8.5), after=(i,))
             tt(xd, xs, rg("DD", a, b), OP.mult)
             tt(rg("HN", a, b), rg("HF", a, b), xd, OP.subtract)
             cp(rg("HS%d" % t, a, b), rg("HN", a, b))
-            send("mH%d_%d" % (t, c))
+            for j, (lo, hi) in enumerate(HM):
+                if hi == b:
+                    send("mH%d_%d" % (t, j))
             tt(rg("AN", a, b), rg("AF", a, b), xd, OP.add)
-            ts(y, sr, 9.0, OP.is_lt, 8192.0, OP.mult)
-            tt(rg("V", a, b), rg("AN", a, b), y, OP.subtract)
-            sca(rg("VW%d" % t), f, rg("V", a, b))
-            tt(rg("AM", a, b), rg("AMF", a, b), xd, OP.add)
-            tt(rg("U", a, b), rg("AM", a, b), y, OP.add)
+            sca(rg("VW%d" % t), f, rg("AN", a, b), rg("QS", a, b), OP.add)
         else:
-            ts(rg("FLG", a, b), sr, 9.0, OP.is_ge)
+            ts(sw, z, rg("TH2"), OP.is_gt)
+            mm(sr, [(rg("BLK"), sw, 128)])
+            act(rg("FLG", a, b), sr, AF.Sign, 1.0, -8.5)
             sca(rg("VF"), f, rg("FLG", a, b))
-            tt(rg("XDF", a, b), rg("SW", a, b), rg("DD", a, b), OP.mult)
+            tt(rg("XDF", a, b), rg("VT", a, b), sw, OP.mult)
+            sca(rg("YC"), rg("AL", a // 16, b // 16), rg("AF", a, b), rg("XDF", a, b), OP.add)
+            sca(rg("YC"), rg("AL", 16 + a // 16, 16 + b // 16), rg("HF", a, b), rg("XDF", a, b), OP.subtract)
 
-            def box(base, lst, op):
-                do("v", lambda e: e.tensor_tensor(out=ap(rg("YC")).indirect(T[lst][:, a // 16:b // 16]), in0=T[base][:, a:b], in1=T.XDF[:, a:b], op=op),
-                   [(base, a, b), rg("XDF", a, b), rg(lst)], [rg("YC")], 0.05 + n * SC * CY)
-            box("AF", "AL", OP.add)
-            box("HF", "NL", OP.subtract)
+    def bits(t):
+        n = CH[0][1]
+        s, x = ("SLB", 64, 64 + n), ("SLB", 0, 16)
+        i = mm(s, [(rg("WB"), rg("SW", a, b), 128) for a, b in CH])
+        red(rg("TS"), s)
+        ts(rg("RI"), rg("TS"), FRAC, OP.add)
+        ts(rg("HB"), rg("RI"), rg("TS"), OP.subtract, rg("CC"), OP.is_le)
+        x = ("RL", 0, 16)
+        if t < RO - 1:
+            mm(x, [(rg("IDN"), rg("ILB"), 128), (rg("IDN"), rg("EB"), 128), (rg("SEL16"), rg("SW"), None)], (i,))
+        else:
+            mm(x, [(rg("SEL"), rg("SW"), None)], (i,))
+        return x
 
-    def store(t, a, b):
-        c, d = a // 16, b // 16
-        tt(rg("UI", c, d), ("SLB", 16 * t + c, 16 * t + d), rg("E15", c, d), OP.add)
-        ts(rg("UJ", c, d), rg("UI", c, d), 15, OP.bitwise_and)
-        tt(rg("UK", c, d), rg("UJ", c, d), rg("IL16", c, d), OP.add)
-        cp(rg("XC", c, d), rg("UK", c, d))
-        sca(rg("X"), rg("XC", c, d), rg("PFB", a, b))
+    def store(x):
+        tt(rg("MW"), x, rg("LIM"), OP.is_ge)
+        tt(rg("XW"), x, rg("MW"), OP.subtract)
+        ts(rg("XC"), rg("XW"), 16.0, OP.mult)
+        sca(rg("X"), rg("XC"), rg("PFB"))
 
-    def xor_list():
-        s, x = ("SLB", 64, 65), ("RL", 64, 96)
-        do("p", [mmf(s, rg("ONF"), ("RS", c, c + 1), c == 0, c == len(CH) - 1) for c in range(len(CH))], [rg("ONF"), ("RS", 0, len(CH))], [s], 1024 * PE)
-        ts(rg("HBI"), s, rg("PWS"), OP.mult, rg("ADS"), OP.add)
-        ts(rg("HBJ"), rg("HBI"), 1, OP.bitwise_and)
-        tt(rg("HBF"), rg("HBJ"), rg("PW"), OP.mult)
-        ts(rg("LH"), rg("LP"), rg("HBF"), OP.mult)
-        do("p", [mmf(x, rg("IDN"), rg("VC"), True, False), mmf(x, rg("IDN"), rg("VLO"), False, False), mmf(x, rg("LH"), rg("RP"), False, True, 9)],
-           [rg("IDN"), rg("VC"), rg("VLO"), rg("LH"), rg("RP")], [x], 192 * PE)
-        cp(rg("XL"), x)
-        cp(rg("XI"), x)
+    def partners(t, x):
+        e = ("SLB", 0, 16)
+        tt(rg("LOW"), x, rg("LF"), OP.is_lt)
+        ts(rg("RH"), rg("FB"), rg("HB"), OP.mult)
+        mm(e, [(rg("IDN"), rg("FH"), 128), (rg("K1024"), rg("LOW"), 128), (rg("SEL"), rg("RH"), None)])
+        ts(rg("EU"), e, 512.0, OP.min)
 
-    def partners(t):
-        gat(rg("AX"), rg("VW%d" % t), rg("XL"))
-
-        def half(a, b):
-            o = rg("WI", a, b)
-            off = T["FU%d" % t][:, a // 16:b // 16]
-            do("v", lambda e: e.tensor_tensor(out=ap(o), in0=ap(rg("AX")).indirect(off), in1=T.U[:, a:b], op=OP.max),
-               [rg("AX"), rg("FU%d" % t), rg("U", a, b)], [o], 0.05 + (b - a) * GA * CY)
-        for j, (a, b) in enumerate(AH):
-            half(a, b)
+        def part(a, b):
+            o, off = rg("WI", a, b), rg("EU", a // 16, b // 16)
+            do("v", lambda e: e.tensor_tensor(out=ap(o), in0=ap(rg("VW%d" % t)).indirect(ap(off)), in1=T.AN[:, a:b], op=OP.max),
+               [rg("VW%d" % t), off, rg("AN", a, b)], [o], 0.05 + (b - a) * GA * CY)
+        for j, (a, b) in enumerate(AM):
+            part(a, b)
             ts(rg("WJ", a, b), rg("WI", a, b), 4095, OP.bitwise_and)
             cp(rg("AS%d" % t, a, b), rg("WJ", a, b))
             send("mA%d_%d" % (t, j))
 
     def sites(t, out):
-        row = "VF"
+        ls = "LS%d" % t
+        row = rg("VF")
         if t < RO - 1:
-            ts(rg("VB"), rg("VW%d" % t), 0.0, OP.is_ge)
-            row = "VB"
-        rowlist(("RL", 256, 288), row, 0, 512)
-        ts(rg("VLB", 0, 32), ("RL", 256, 288), 0.0625, OP.mult)
-        cp(rg("VLB", 32, 64), rg("LS%d" % t, 32, 64))
-        ts(rg("XK"), rg("XI", 0, 1), 15, OP.bitwise_and)
-        cp(rg("XKF"), rg("XK"))
-        ts(rg("PM"), rg("M16B"), rg("XKF"), OP.is_equal)
-        ts(rg("XJ"), rg("XI"), 4, OP.arith_shift_right)
-        tt(rg("XM"), rg("XJ"), rg("DM"), OP.mult)
+            row = rg("VB")
+            act(row, rg("VW%d" % t, 0, 512), AF.Sign)
+        z = "Z0"
+        mm((z, 384, 416), [(rg("SEL"), row, None)])
+        ts(rg(ls, 64, 96), (z, 384, 416), 0.0, OP.is_gt)
+        ts(rg("LH"), rg("BITS", 512, 640), rg("HB"), OP.mult)
+        z = "Z1"
+        mm((z, 384, 512), [(rg("ONE"), rg("LH"), 4)])
+        mm((z, 320, 324), [(rg("IDN"), rg("J4", 0, 4), 128), (rg("LH"), rg("RP2", 0, 4), 9)])
+        cp(rg("HLU"), (z, 320, 324))
+        tt(rg("PM"), (z, 384, 512), rg("NCM"), OP.is_equal)
+        gat(rg("GXL"), rg(ls, 32, 96), rg("HLU"))
+        mm((z, 320, 384), [(rg("PM"), rg("GXL"), 128)])
+        tt(rg("BO"), (z, 352, 384), rg(ls, 64, 96), OP.mult)
+        tt(rg("BD"), (z, 320, 352), rg(ls, 32, 64), OP.subtract)
+        tt(rg("BE"), rg("BO"), rg("BD"), OP.mult)
+        tt(out, rg("BE"), rg(ls, 32, 64), OP.add)
 
-        def half(j):
-            do("v", lambda e: e.tensor_reduce(T.HL[:, j:j + 1], T.XM[:, 16 * j:16 * j + 16], AxisListType.X, OP.add), [rg("XM")], [("HL", j, j + 1)], el(16))
-        half(0)
-        half(1)
-        cp(rg("HLU"), rg("HL", 0, 2))
-        gat(rg("GXL", 0, 32), rg("VLB", 0, 32), rg("HLU"))
-        gat(rg("GXL", 32, 64), rg("VLB", 32, 64), rg("HLU"))
-        do("p", mmf(("RL", 320, 384), rg("PM"), rg("GXL"), True, True), [rg("PM"), rg("GXL")], [("RL", 320, 384)], 64 * PE)
-        tt(rg("BO"), rg("VLB", 0, 32), ("RL", 320, 352), OP.mult)
-        tt(rg("BD"), ("RL", 352, 384), rg("VLB", 32, 64), OP.subtract)
-        if t == 0:
-            tt(out, rg("BO"), rg("BD"), OP.mult)
+    def turns(t, x):
+        if t < RO - 1:
+            tt(rg("TL"), x, rg("LT"), OP.is_lt)
         else:
-            tt(rg("BD"), rg("BO"), rg("BD"), OP.mult)
-            tt(out, rg("BD"), rg("VLB", 32, 64), OP.add)
-
-    def turns(t):
-        ts(rg("TL"), ("SLB", 16 * t, 16 * t + 16), 4.0, OP.is_le)
-        tt(rg("DFG"), rg("LS%d" % t, 16, 32), rg("LS%d" % t, 0, 16), OP.subtract)
-        if t == 0:
-            tt(rg("DL0", 0, 16), rg("TL"), rg("DFG"), OP.mult)
-            ts(rg("DL0", 16, 32), rg("DL0", 0, 16), -1.0, OP.mult)
-            return
+            ts(rg("TL"), x, 4.0, OP.is_le)
         tt(rg("TD"), rg("TL"), rg("DFG"), OP.mult)
         if t < RO - 1:
             tt(rg("LO%d" % t, 0, 16), rg("LS%d" % t, 0, 16), rg("TD"), OP.add)
             tt(rg("LO%d" % t, 16, 32), rg("LS%d" % t, 16, 32), rg("TD"), OP.subtract)
         else:
             tt(rg("YF"), rg("LS%d" % t, 0, 16), rg("TD"), OP.add)
-            dma("y", T.yf[:], T.YF[:], "yf", [rg("YF")], [], 8192)
-            tt(rg("DAN"), rg("ALF"), rg("NLF"), OP.subtract)
+            dma("y", T.yf[:], T.YF[:], "yf", [rg("YF")], [], 2.3)
             tt(rg("TA"), rg("TL"), rg("DAN"), OP.mult)
-            tt(rg("YN"), rg("NLF"), rg("TA"), OP.add)
-            dma("y", T.yn[:], T.YN[:], "yn", [rg("YN")], [], 8192)
+            tt(rg("YN"), rg("LB", 16, 32), rg("TA"), OP.add)
+            dma("y", T.yn[:], T.YN[:], "yn", [rg("YN")], [], 2.3)
 
-    last = len(CH) - 1
     start()
     for t in range(RO):
-        for role in ("H", "A"):
-            for c, (a, b) in enumerate(CH):
-                frames(role, t, a, b)
-                maxima(role, a, b)
-                sums(role, c, a, b)
-        take(t)
+        parts = [("H", a, b) for a, b in HC] + [("A", a, b) for a, b in CH] if t else [(role, a, b) for a, b in CH for role in "HA"]
+        for role, a, b in parts:
+            frames(role, t, a, b)
+            maxima(role, a, b)
+            for c, (lo, hi) in enumerate(CH):
+                if a <= lo < b:
+                    sums(role, c, lo, hi)
+        take_nurses(t)
+        for a, b in AM:
+            take_flyers(t, a, b)
         take_lists(t)
-        if t == RO - 1:
-            boxes_of_sites()
-        for c in range(last):
+        for c in range(len(CH)):
             decide(t, c)
+        x = bits(t)
         if t < RO - 1:
-            store(t, 0, CH[last][0])
-        decide(t, last)
-        if t < RO - 1:
-            store(t, CH[last][0], P)
-        xor_list()
-        if t < RO - 1:
-            partners(t)
-            turns(t)
-            sites(t, rg("DL0" if t == 0 else "LO%d" % t, 32, 64))
+            store(x)
+            partners(t, x)
+            turns(t, x)
+            sites(t, rg("LO%d" % t, 32, 64))
             send("mL%d" % t)
+            if t == RO - 2:
+                boxes()
         else:
-            dma("y", T.yc[:], T.YC[:], "yc", [rg("YC")], [], 262144)
+            dma("y", T.yc[:], T.YC[:], "yc", [rg("YC")], [], 3.4)
             sites(t, rg("YB"))
-            dma("s", T.yb[:], T.YB[:], "yb", [rg("YB")], [], 16384)
-            turns(t)
-    for o in arrange(ops):
+            dma("s", T.yb[:], T.YB[:], "yb", [rg("YB")], [], 2.3)
+            turns(t, x)
+    for o in ops[:len(LOADS)] + [o for o in arrange(ops) if not (o["kind"] == "dma" and not o["rd"])]:
         issue(o)
 
-    for sem, val in list(cnt.items()) + list(total.items()):
-        wait("g", sem, val, {})
+    for sem, n in list(cnt.items()) + list(total.items()):
+        wait("g", sem, n, {})
     g.wait_ge(T.sem.loc, NE * len(MSGS))

@@ -4,12 +4,19 @@ P, WX, RO = 256, 4096, 3
 CH = [(0, 64), (64, 128), (128, 192), (192, 256)]
 HC = CH
 HM = CH
-AM = [(0, 64), (64, 256)]
-NE = 8
+AM = [(0, 128), (128, 256)]
+ST = [(0, 256)]
+PASSES, NV, NG, IP = 1, 10, 4, 512
+YS = [(0, 192), (192, 256)]
+QR, LATE, NR, BX, QI, QF = "v", 3, 1, False, "s", "s"
+VG = {(t, r, 0): 32 for t in range(RO) for r in "HA"}
+KB, SB, SF, QT = 1, 0, 1, "vvs"
+ORDER = []
+LN2 = 0.6931471805599453
 FRAC = -0.5 + 2.0 ** -10
 SH = 25.0 / 64
 BIG = 1.5 * 2.0 ** 27
-CY, GA, SC, PE, WK, HOP = 0.00083, 1.56, 3.8, 0.00042, 0.16, 7.0
+CY, GA, SC, PE, WK, HOP, FIRST, RATE = 0.00083, 1.7, 3.8, 0.00042, 0.22, 6.0, 2.0, 250e3
 
 SCRATCH = {}
 
@@ -21,22 +28,22 @@ def _sb(name, cols, dtype="float32"):
 for _d, _l in (
         ("bfloat16", "X:4096 PFB:256 PNB:256 CF:4096 CN:4096 GH:4096 GA:4096 OHF:4096 OHN:4096 OAF:4096 OAN:4096 KHF:256 KHN:256 KAF:256 KAN:256 "
                      "SEL:144 NSEL:144 SEL16:144 ONE:128 BLK0:128 BLK:128 IDN:128 BR:128 K1024:128 WB0:128 WB:128 BITS:640 RP0:16 RP1:16 RP2:16 J4:16 "
-                     "ILB:16 EB:16 SW:256 FB:256 RH:256 LOW:16 LH:128 PM:128 VB:512 VF:512 FLG:256"),
+                     "PW:1 PR:1 ILB:16 EB:16 SW:256 FB:256 RH:256 LOW:16 LH:128 BLKQ:128 CQ:128 VB:512 VF:512 FLG:256"),
         ("int32", "CBI:512 BSI:32 FSI:16 NBI:16 THI:1 CS:512 BI:640 BJ:640 WI:256 WJ:256"),
-        ("uint16", "LU0:64 FG:32 AL:32 XC:16 EU:16 HLU:4"),
-        ("float16", "GROW:256 FH:16 EF:512 NROW:512 GXL:64"),
-        ("float32", "M16:128 MB0:128 M16B:128 NCM:128 D0:128 D1:128 WR:128 IOV:640 IC16:16 INV:512 BROW:512 LA:32 LB:32 "
-                    "HF:256 AF:256 DD:256 HN:256 AN:256 QS:256 XDF:256 YC:512 YB:32 YF:16 YN:16 VW0:528 VW1:528")):
+        ("uint16", "LU0:64 AL:32 XC:16 EU:16 HLU:4"),
+        ("float16", "GROW:256 FH:16 EF:512 NROW:512"),
+        ("float32", "M16:128 MB0:128 M16B:128 NCM:128 IOV:640 IC16:16 INV:512 BROW:512 HF:256 HN:256 "
+                    "PM:128 GXL:64 AF:256 DD:256 AN:256 QS:256 XDF:256 YC:512 YB:32 YF:16 YN:16 VW0:528 VW1:528 VW2:512")):
     for _e in _l.split():
         _sb(_e.split(":")[0], int(_e.split(":")[1]), _d)
 for _t in range(RO):
-    for _n, _c, _d in [("AU", 256, "uint16"), ("HU", 256, "uint16"), ("LS", 96, "float32"), ("FU", 16, "uint16")]:
+    for _n, _c, _d in [("AU", 288, "uint16"), ("HU", 256, "uint16"), ("LS", 128, "float32")]:
         _sb(_n + str(_t), _c, _d)
     if _t < RO - 1:
-        for _n, _c, _d in [("AS", 256, "uint16"), ("HS", 256, "uint16"), ("LO", 64, "float32")]:
+        for _n, _c, _d in [("AS", 288, "uint16"), ("HS", 256, "uint16"), ("LO", 128, "float32")]:
             _sb(_n + str(_t), _c, _d)
 ALIAS = {}
-for _k, _d, _l in (("KF", "float32", "PL:1 PWH:1 PW:1 PR:1 P9:1 P2:1 NP2:1 CC:1 TH2:1 TS:1 HB:1 DM:16 DW:16 IL:16 E16:16 LB0:16 LIM:16 LT:16 LF:16 "
+for _k, _d, _l in (("KF", "float32", "PL:1 P2:1 NP2:1 CC:1 TH2:1 TS:1 HB:1 DM:16 IL:16 E16:16 LB0:16 LIM:16 LT:16 LF:16 "
                                      "MW:16 XW:16 TL:16 DFG:16 TD:16 DAN:16 TA:16 BO:32 BD:32 BE:32"),
                    ("KI", "int32", "EI:16 EJ:16 PI:1 PJ:1 RI:1")):
     _o = 0
@@ -51,46 +58,40 @@ for _n in PS:
 MSGS = []
 for _t in range(RO - 1):
     MSGS += [("mH%d_%d" % (_t, _c), "HS%d" % _t, "HU%d" % (_t + 1), _a, _b) for _c, (_a, _b) in enumerate(HM)]
-    MSGS += [("mA%d_%d" % (_t, _c), "AS%d" % _t, "AU%d" % (_t + 1), _a, _b) for _c, (_a, _b) in enumerate(AM)]
-    MSGS += [("mL%d" % _t, "LO%d" % _t, "LS%d" % (_t + 1), 0, 64)]
-MSGS += [("mB", "LA", "LB", 0, 32)]
+    MSGS += [("mA%d_%d" % (_t, _c), "AS%d" % _t, "AU%d" % (_t + 1), _a and 32 + _a, 32 + _b) for _c, (_a, _b) in enumerate(AM)]
+    MSGS += [("mL%d" % _t, "LO%d" % _t, "LS%d" % (_t + 1), 64, 96 if _t < RO - 2 else 128)]
 LOADS = [("y", "NBI", "nb"), ("s", "PFB", "pf"), ("y", "BSI", "bs"), ("s", "PNB", "pn"), ("y", "CBI", "cb"), ("s", "FSI", "fs"), ("y", "X", "xf"), ("s", "THI", "th")]
 OUTS = ["yc", "yb", "yf", "yn"]
 SEMAPHORES = ["sv", "ss", "sp", "sg", "loc"] + [m[0] for m in MSGS] + ["d" + n[1] for n in LOADS] + ["d" + n for n in OUTS]
 
 
-def hop(core, dst, topo, T):
+def hop(core, dst, topo, T, j):
     if topo.may_write(core, dst):
         return core
-    own = [c for c in topo.cores_of(core) if T.rank_of(c) is None and topo.may_write(c, dst)]
-    return [c for c in own if topo.die(c) == topo.die(core)][0]
-
-
-def mask_of(src, dst, topo):
-    m = 0
-    for e in topo.engines(src, dst)[:NE]:
-        m |= 1 << e
-    return m
+    own = [c for c in topo.cores_of(core) if T.rank_of(c) is None and topo.may_write(c, dst) and topo.die(c) == topo.die(core)][:NR]
+    return own[j % len(own)]
 
 
 def put(g, T, topo, src, dst, out, in_, sem):
     rid, pid = topo.addr(dst, src)
-    g.remote_dma(out_ap=out, in_ap=in_, remote_sem=T.sem[sem], local_sem=T.sem.loc, pid=pid, routing_id=rid, dma_engine_mask=mask_of(src, dst, topo))
+    g.remote_dma(out_ap=out, in_ap=in_, remote_sem=T.sem[sem], local_sem=T.sem.loc, pid=pid, routing_id=rid, dma_engine_mask=topo.mask(src, dst))
 
 
 def relay_program(g, core, T, topo):
     for r, c in enumerate(T.cores):
         dst = T.cores[(r + 1) % len(T.cores)]
-        if c in topo.cores_of(core) and hop(c, dst, topo, T) == core:
-            for sem, _, land, a, b in MSGS:
-                g.wait_ge(T.sem[sem], NE)
-                put(g, T, topo, core, dst, T[land][:, a:b], T[land][:, a:b], sem)
-            g.wait_ge(T.sem.loc, NE * len(MSGS))
+        mine = [m for j, m in enumerate(MSGS) if c in topo.cores_of(core) and hop(c, dst, topo, T, j) == core]
+        for sem, _, land, a, b in mine:
+            g.wait_ge(T.sem[sem], len(topo.engines(c, core)))
+            put(g, T, topo, core, dst, T[land][:, a:b], T[land][:, a:b], sem)
+        if mine:
+            g.wait_ge(T.sem.loc, len(topo.engines(core, dst)) * len(mine))
 
 
 def arrange(ops):
     n = len(ops)
     pred = [set(o["after"]) for o in ops]
+    feeds = set()
     hist = {}
     for i, o in enumerate(ops):
         for group, w in ((o["rd"], False), (o["wr"], True)):
@@ -98,6 +99,7 @@ def arrange(ops):
                 for j, jlo, jhi, jw in hist.get(name, []):
                     if j != i and jlo < hi and lo < jhi and (w or jw):
                         pred[i].add(j)
+                        feeds.add((j, i))
         for group, w in ((o["rd"], False), (o["wr"], True)):
             for name, lo, hi in group:
                 old = hist.get(name, [])
@@ -110,25 +112,46 @@ def arrange(ops):
             succ[j].append(i)
 
     def lag(i, j):
-        return 0.0 if ops[i]["q"] == "p" and ops[j]["q"] == "p" else WK
+        return 0.0 if ops[i]["q"] == ops[j]["q"] and (ops[i]["q"] == "p" or (i, j) not in feeds) else WK
     rank = [0.0] * n
     for i in range(n - 1, -1, -1):
         rank[i] = ops[i]["cost"] + max([rank[j] + lag(i, j) for j in succ[i]] + [0.0])
-    start = [0.0] * n
-    taken = {}
-    for i in sorted(range(n), key=lambda i: (-rank[i], i)):
-        st = max([start[j] + ops[j]["cost"] + lag(j, i) for j in pred[i]] + [0.0])
-        hold = ops[i]["hold"]
-        if hold:
-            line = taken.setdefault(ops[i]["q"], [])
-            for lo, hi in line:
-                if st + hold <= lo:
-                    break
-                st = max(st, hi)
-            line.append((st, st + hold))
-            line.sort()
-        start[i] = st
-    return [ops[i] for i in sorted(range(n), key=lambda i: (start[i], i))]
+    banks = [set(r[0] for r in o["rd"] + o["wr"] if r[0] in PS) for o in ops]
+
+    def place(order, back):
+        start = [0.0] * n
+        taken = {}
+        for i in order:
+            o = ops[i]
+            hold, q = o["hold"], o["q"]
+            if back:
+                st = max([start[j] + lag(i, j) + o["cost"] - hold for j in succ[i]] + [o["cost"] - hold])
+            else:
+                st = max([start[j] + ops[j]["cost"] + lag(j, i) for j in pred[i]] + [0.0])
+            moved = hold > 0
+            while moved:
+                moved = False
+                for name in [q] + sorted(banks[i]):
+                    for lo, hi, who in taken.get(name, []):
+                        gap = 0.0 if who == q else WK
+                        if (name == q or who != q) and lo - gap < st + hold - 1e-9 and st < hi + gap - 1e-9:
+                            st, moved = hi + gap, True
+            if hold:
+                for name in [q] + sorted(banks[i]):
+                    taken.setdefault(name, []).append((st, st + hold, q))
+                    taken[name].sort()
+            start[i] = st + hold if back else st
+        return start
+
+    start = place(sorted(range(n), key=lambda i: (-rank[i], i)), False)
+    best = None
+    for _ in range(PASSES):
+        back = place(sorted(range(n), key=lambda i: (-start[i] - ops[i]["hold"], -i)), True)
+        start = place(sorted(range(n), key=lambda i: (-1e9 if ops[i]["first"] else -back[i], i)), False)
+        end = max(start[i] + ops[i]["cost"] for i in range(n))
+        if best is None or end < best[0]:
+            best = (end, start)
+    return sorted(range(n), key=lambda i: (-1.0 if ops[i]["first"] else best[1][i], i))
 
 
 def rank_program(g, core, T, topo):
@@ -137,7 +160,9 @@ def rank_program(g, core, T, topo):
         relay_program(g, core, T, topo)
         return
     nxt = T.cores[(rank + 1) % len(T.cores)]
-    via = hop(core, nxt, topo, T)
+    via = [hop(core, nxt, topo, T, j) for j in range(len(MSGS))]
+    via = [nxt if c == core else c for c in via]
+    NE = len(topo.engines(hop(T.cores[rank - 1], core, topo, T, 0), core))
 
     Q = {"v": g.vector, "s": g.scalar, "p": g.tensor, "g": g, "y": g.sync}
     QS = {"v": "sv", "s": "ss", "p": "sp", "g": "sg"}
@@ -145,8 +170,8 @@ def rank_program(g, core, T, topo):
     known = {q: {} for q in Q}
     acc = {}
     total = {}
-    ops = []
-    read = []
+    ops, table = [], []
+    read, swept, last, nurses, flyers, wiped, spreads, summed, stored = [], [], [], [], [], [], [], [], []
 
     def wait(q, sem, val, know):
         k = known[q]
@@ -189,7 +214,8 @@ def rank_program(g, core, T, topo):
                 acc[name] = keep + [(lo, hi, w, q, sem, val, dma, know)]
 
     def add(kind, q, fns, rd, wr, cost, hold=None, after=(), extra=None):
-        ops.append({"kind": kind, "q": q, "fns": fns, "rd": rd, "wr": wr, "cost": cost, "hold": cost if hold is None else hold, "after": after, "extra": extra})
+        ops.append({"kind": kind, "q": q, "fns": fns, "rd": rd, "wr": wr, "cost": cost, "hold": cost if hold is None else hold, "after": after, "extra": extra,
+                    "first": kind == "dma" and not rd})
         return len(ops) - 1
 
     def do(q, fns, rd, wr, cost, after=()):
@@ -200,8 +226,9 @@ def rank_program(g, core, T, topo):
 
     def send(sem):
         _, src, land, a, b = [m for m in MSGS if m[0] == sem][0]
-        i = add("send", "g", None, [(src, a, b)], [("SENDQ", 0, 1)], 1.0, 1.0, (), sem)
-        add("land", "r", None, [], [(land, a, b)], HOP - 1.0, 0.0, (i,), sem)
+        more = FIRST if sem == MSGS[0][0] else 0.0
+        i = add("send", "g", None, [(src, a, b)], [("SENDQ", 0, 1)], 1.0 + more, 1.0 + more, (), sem)
+        add("land", "r", None, [], [(land, a, b)], HOP - 1.0 + more, 0.0, (i,), sem)
 
     def issue(o):
         q = o["q"]
@@ -219,8 +246,7 @@ def rank_program(g, core, T, topo):
         elif o["kind"] == "send":
             m = [m for m in MSGS if m[0] == o["extra"]][0]
             deps("g", o["rd"], [])
-            dst, out = (nxt, m[2]) if via == core else (via, m[2])
-            put(g, T, topo, core, dst, T[out][:, m[3]:m[4]], T[m[1]][:, m[3]:m[4]], m[0])
+            put(g, T, topo, core, via[MSGS.index(m)], T[m[2]][:, m[3]:m[4]], T[m[1]][:, m[3]:m[4]], m[0])
         else:
             land, a, b = o["wr"][0]
             acc.setdefault(land, []).append((a, b, True, "r", o["extra"], NE, True, {}))
@@ -255,9 +281,9 @@ def rank_program(g, core, T, topo):
             return do("v", lambda e: e.tensor_scalar(out=ap(o), in0=ap(x), scalar1=val(s1), scalar2=None, op0=op0), rd, [o], c)
         return do("v", lambda e: e.tensor_scalar(out=ap(o), in0=ap(x), scalar1=val(s1), scalar2=val(s2), op0=op0, op1=op1), rd, [o], c)
 
-    def cp(o, x, out=None, in_=None, n=None):
+    def cp(o, x, out=None, in_=None, n=None, after=()):
         w, r = out if out is not None else ap(o), in_ if in_ is not None else ap(x)
-        do("v", lambda e: e.tensor_copy(out=w, in_=r), [x], [o], el(n or x[2] - x[1], 0.5 if two(o) and two(x) else 1.0))
+        do("v", lambda e: e.tensor_copy(out=w, in_=r), [x], [o], el(n or x[2] - x[1], 0.5 if two(o) and two(x) else 1.0), after)
 
     def act(o, x, func=AF.Copy, scale=1.0, bias=None, out=None, n=None, after=()):
         w = out if out is not None else ap(o)
@@ -265,6 +291,12 @@ def rank_program(g, core, T, topo):
         if bias is None:
             return do("s", lambda e: e.activation(w, ap(x), func, scale=scale), [x], [o], c, after)
         return do("s", lambda e: e.activation(w, ap(x), func, bias=bias, scale=scale), [x], [o], c, after)
+
+    def scaled(o, x, col, q):
+        if q == "v":
+            ts(o, x, col, OP.mult)
+        else:
+            do("s", lambda e: e.activation(ap(o), ap(x), AF.Copy, scale=ap(col)), [x, col], [o], (x[2] - x[1]) * CY + 0.05)
 
     def red(o, x):
         do("v", lambda e: e.tensor_reduce(ap(o), ap(x), AxisListType.X, OP.add), [x], [o], el(x[2] - x[1]))
@@ -279,9 +311,12 @@ def rank_program(g, core, T, topo):
         else:
             return do("s", lambda e: e.activation(ap(o), ap(win).indirect(ap(off)), AF.Copy), [win, off], [o], c, after)
 
-    def sca(win, off, x, y=None, op=None):
+    def sca(win, off, x, y=None, op=None, q="v"):
         c = 0.05 + (x[2] - x[1]) * SC * CY
-        if y is None:
+        if q == "s":
+            do("s", lambda e: e.activation(ap(win).indirect(ap(off)), ap(x), AF.Silu), [x, off], [win], c + (0.0 if table else 1.5))
+            table.append(1)
+        elif y is None:
             do("v", lambda e: e.tensor_copy(out=ap(win).indirect(ap(off)), in_=ap(x)), [x, off], [win], c)
         else:
             do("v", lambda e: e.tensor_tensor(out=ap(win).indirect(ap(off)), in0=ap(x), in1=ap(y), op=op), [x, y, off], [win], c)
@@ -299,8 +334,9 @@ def rank_program(g, core, T, topo):
             return lambda e: e.matmul(ap(o), fl[i][0], fl[i][1], i == 0, i == len(fl) - 1)
         return do("p", [one(i) for i in range(len(fl))], rd, [o], len(fl) * max(64, o[2] - o[1]) * PE, after)
 
-    def aff(o, x, pat, op, fillv, base, cm):
-        do("g", lambda e: e.affine_select(ap(o), ap(x), pat, op, fillv, base, cm), [x], [o], 0.17 + 2 * (o[2] - o[1]) * CY)
+    def aff(o, x, pat, op, fillv, base, cm, out=None):
+        w = out if out is not None else ap(o)
+        do("g", lambda e: e.affine_select(w, ap(x), pat, op, fillv, base, cm), [x], [o], 0.17 + 2 * (x[2] - x[1]) * CY)
 
     def iota(o, pat, base, cm, flag=True):
         do("g", (lambda e: e.iota(ap(o), pat, base, cm, allow_small_or_imprecise_dtypes=True)) if flag else (lambda e: e.iota(ap(o), pat, base, cm)),
@@ -310,9 +346,11 @@ def rank_program(g, core, T, topo):
         size = 0
         for q, n, src in LOADS:
             size += 128 * SCRATCH[n][1][1] * (2 if two(rg(n)) else 4)
-            dma(q, T[n][:], T[src][:], n, [], [rg(n)], 2.2 + size / 220e3)
-        for n, c in (("ONE", 1.0), ("SEL", 0.0), ("VW0", -16384.0), ("VW1", -16384.0), ("VF", -1.0)):
+            dma(q, T[n][:], T[src][:], n, [], [rg(n)], 2.2 + size / RATE)
+        for n, c in (("ONE", 1.0), ("SEL", 0.0), ("CQ", 8192.0 * (16 * SH - 8.5))):
             fill(rg(n), c)
+        for n, c in (("VW0", -16384), ("VW1", -16384), ("VW2" if QF == "s" else "VF", -1)):
+            iota(rg(n), [[0, rg(n)[2]]], c, 0)
         aff(rg("BLK0"), rg("ONE"), [[-16, 8], [0, 16]], OP.is_ge, 0.0, 0, 1)
         aff(rg("BLK"), rg("BLK0"), [[16, 8], [0, 16]], OP.is_ge, 0.0, 15, -1)
         aff(rg("IDN"), rg("ONE"), [[-1, 128]], OP.is_equal, 0.0, 0, 1)
@@ -322,37 +360,37 @@ def rank_program(g, core, T, topo):
         ts(rg("K1024"), rg("IDN"), 16.0, OP.mult)
         tt(rg("BR"), rg("K1024"), rg("BLK"), OP.add)
         ts(rg("K1024"), rg("IDN"), 1024.0, OP.mult)
+        ts(rg("BLKQ"), rg("BLK"), 8192.0, OP.mult)
         cp(rg("LU0", 48, 64), rg("NBI"))
         gat(rg("HU0"), rg("CBI"), rg("LU0", 48, 64))
         cp(rg("LU0", 0, 32), rg("BSI"))
         gat(rg("CS"), rg("CBI"), rg("LU0", 0, 32))
-        cp(rg("FU0"), rg("FSI"))
-        gat(rg("AU0"), rg("CS"), rg("FU0"))
-        for k in range(16):
-            cp(("CF", k, k + 1), rg("PFB"), T.CF[:, k:4096:16], T.PFB[:, :])
-            act(("CN", k, k + 1), rg("PNB"), out=T.CN[:, k:4096:16])
-        act(rg("PF", 0, 256), rg("PFB"))
-        act(rg("PF", 256, 512), rg("PNB"))
+        cp(rg("LU0", 32, 48), rg("FSI"))
+        cp(rg("AU0", 0, 16), rg("FSI"))
+        gat(rg("AU0", 32, 288), rg("CS"), rg("LU0", 32, 48))
+        for j in range(32):
+            c, src, k = ("CF", "PFB", j) if j < 16 else ("CN", "PNB", j - 16)
+            if j < NV:
+                cp((c, k, k + 1), rg(src), T[c][:, k:4096:16], T[src][:, :])
+            elif j < 32 - NG:
+                act((c, k, k + 1), rg(src), out=T[c][:, k:4096:16])
+            else:
+                aff((c, k, k + 1), rg(src), [[0, P]], OP.is_ge, 0.0, 0, 0, T[c][:, k:4096:16])
         iota(rg("PI"), [[0, 1]], 0, 1, False)
         iota(rg("M16"), [[0, 8], [1, 16]], 0, 0)
         iota(rg("IC16"), [[16, 16]], 0, 0)
-        iota(rg("IOV", 0, 512), [[1, 512]], 0, 0)
+        iota(rg("IOV", 0, 512), [[1, 512]], 1024, 0)
         iota(rg("IOV", 512, 640), [[0, 8], [17, 16]], 0, 0)
         ts(rg("PJ"), rg("PI"), 15, OP.bitwise_and)
         cp(rg("PL"), rg("PJ"))
         ts(rg("DM"), rg("M16", 0, 16), rg("PL"), OP.is_equal)
-        ts(rg("D0"), rg("M16"), 0.0, OP.not_equal, 0.5, OP.mult)
-        ts(rg("D1"), rg("M16"), 0.0, OP.is_equal, 0.5, OP.mult)
-        do("v", lambda e: e.tensor_tensor_scan(T.WR[:, :], T.D0[:, :], T.D1[:, :], 0.0, OP.mult, OP.add), [rg("D0"), rg("D1")], [rg("WR")], el(128))
-        cp(rg("WB"), rg("WR"))
+        ops[act(rg("PW"), rg("PL"), AF.Exp, -LN2)].update(cost=1.4, hold=1.4)
+        act(rg("PR"), rg("PL"), AF.Exp, LN2)
+        act(rg("WB"), rg("M16"), AF.Exp, -LN2)
         aff(rg("WB0"), rg("WB"), [[0, 8], [1, 16]], OP.is_ge, 0.0, -1, 0)
         aff(rg("WB"), rg("WB0"), [[0, 8], [-1, 16]], OP.is_ge, 0.0, 8, 0)
-        tt(rg("DW"), rg("WR", 0, 16), rg("DM"), OP.mult)
-        red(rg("PWH"), rg("DW"))
-        ts(rg("PW"), rg("PWH"), 2.0, OP.mult)
-        do("v", lambda e: e.reciprocal(ap(rg("PR")), ap(rg("PW"))), [rg("PW")], [rg("PR")], 0.2)
-        ts(rg("P9"), rg("PL"), 9.0, OP.is_lt)
-        tt(rg("P2"), rg("PR"), rg("P9"), OP.mult)
+        ts(rg("WB"), rg("WB"), 0.5, OP.mult)
+        ts(rg("P2"), rg("PL"), 9.0, OP.is_lt, rg("PR"), OP.mult)
         ts(rg("NP2"), rg("P2"), -2.0, OP.mult)
         ts(rg("CC"), rg("PL"), 1.0, OP.min, -0.5, OP.mult)
         ts(rg("BI"), rg("IOV"), rg("PW"), OP.mult, FRAC, OP.add)
@@ -379,29 +417,38 @@ def rank_program(g, core, T, topo):
         ts(rg("LT"), rg("LB0"), 4.5 / 16, OP.add)
         ts(rg("LF"), rg("LB0"), 8.5 / 16, OP.add)
         cp(rg("LS0", 0, 16), rg("FSI"))
-        cp(rg("LS0", 32, 64), rg("BSI"))
-        sca(rg("INV"), rg("LU0", 0, 32), rg("IOV", 0, 512))
+        cp(rg("LS0", 64, 96), rg("BSI"))
+        for a in range(0, 512, IP):
+            sca(rg("INV"), rg("LU0", a // 16, (a + IP) // 16), rg("IOV", a, a + IP), q=QI)
         gat(rg("GROW"), rg("INV"), rg("LU0", 48, 64))
         mm(rg("RL", 16, 32), [(rg("SEL16"), rg("GROW"), None)])
-        cp(rg("LS0", 16, 32), rg("RL", 16, 32))
+        ts(rg("LS0", 16, 32), rg("RL", 16, 32), -1024.0, OP.add)
 
     def frames(role, t, a, b):
-        read[:] = [gat(("G" + role, 16 * a, 16 * b), rg("X"), rg(role + "U%d" % t, a, b), "s", tuple(read))]
+        o = 32 * (role == "A")
+        n = VG.get((t, role, a), 0)
+        if n:
+            gat(("G" + role, 16 * a, 16 * (a + n)), rg("X"), rg(role + "U%d" % t, o + a, o + a + n))
+            a += n
+        read[:] = [gat(("G" + role, 16 * a, 16 * b), rg("X"), rg(role + "U%d" % t, o + a, o + b), "s", tuple(read))]
 
     def maxima(role, a, b):
         gx = ("G" + role, 16 * a, 16 * b)
         row0 = T["G" + role][:, 16 * a:16 * b:16]
 
-        def first(f, o):
-            k = ("K" + role + f, a, b)
-            do("v", lambda e: e.tensor_tensor(out=ap(k), in0=row0, in1=T.PF[:, o + a:o + b], op=OP.max), [gx, ("PF", o + a, o + b)], [k], el(b - a))
+        o = 256 * (role == "A")
+        kept = ("PF", o + a, o + b)
+        do("p", lambda e: e.matmul(ap(kept), T.IDN[:, :], row0, True, True), [rg("IDN"), gx], [kept], max(64, b - a) * PE, tuple(spreads))
+
+        def first(f, src):
+            swept.extend([tt(("K" + role + f, a, b), kept, rg(src, a, b), OP.max)][:KB])
 
         def rest(f, c, lo, hi):
             o, d, x = ("O" + role + f, lo, hi), (c, lo, hi), (gx[0], lo, hi)
-            do("v", lambda e: e.tensor_tensor_scan(ap(o), ap(d), ap(x), 255.0, OP.min, OP.max), [x, rg(c)], [o], el(hi - lo, 0.5))
-        first("F", 0)
-        first("N", 256)
-        do("v", lambda e: e.memset(row0, 255.0), [], [gx], el(b - a, 0.5))
+            swept[:] = [do("v", lambda e: e.tensor_tensor_scan(ap(o), ap(d), ap(x), 255.0, OP.min, OP.max), [x, rg(c)], [o], el(hi - lo, 0.5), tuple(swept))]
+        wiped[:] = [do("v", lambda e: e.memset(row0, 255.0), [], [gx], el(b - a, 0.5))]
+        first("F", "PFB")
+        first("N", "PNB")
         for lo, hi in CH:
             if a <= lo < b:
                 rest("F", "CF", 16 * lo, 16 * hi)
@@ -410,63 +457,61 @@ def rank_program(g, core, T, topo):
     def sums(role, c, a, b):
         z = ("Z%d" % c, 0, b - a)
 
-        def one(f, k):
+        def one(f, k, last):
             neg = (role == "H") == (f == "F")
             rhs = T["O" + role + f][:, 16 * a + k:16 * b:16] if k else T["K" + role + f][:, a:b]
-            return lambda e: e.matmul(ap(z), T["NSEL" if neg else "SEL"][:, 15 - k:143 - k], rhs, role == "H" and f == "F" and k == 0, role == "A" and f == "N" and k == 15)
+            return lambda e: e.matmul(ap(z), T["NSEL" if neg else "SEL"][:, 15 - k:143 - k], rhs, role == "H" and f == "F" and k == 1, role == "A" and last)
         for f in ("F", "N"):
-            do("p", [one(f, k) for k in range(16)], [rg("NSEL"), rg("SEL"), ("O" + role + f, 16 * a, 16 * b), ("K" + role + f, a, b)],
-               [(z[0], 0, 512) if (role, f) == ("H", "F") else z], 16 * max(64, b - a) * PE)
+            rows = [one(f, k, f == "N" and k == 15) for k in range(1, 16)]
+            summed[:] = [do("p", rows, [rg("NSEL"), rg("SEL"), ("O" + role + f, 16 * a, 16 * b)], [(z[0], 0, 512) if (role, f) == ("H", "F") else z],
+                            15 * max(64, b - a) * PE, tuple(summed))][:SB]
+            if f == "F":
+                do("p", [one("F", 0, False), one("N", 0, False)], [rg("NSEL"), rg("SEL"), ("K" + role + "F", a, b), ("K" + role + "N", a, b)], [z], 2 * max(64, b - a) * PE)
 
     def boxes():
         lo = "LO%d" % (RO - 2)
 
         def spread(l):
-            do("v", lambda e: e.tensor_scalar(out=T.EF[:, l:512:16], in0=T[lo][:, 32:64], scalar1=ap(rg("DM", l, l + 1)), scalar2=None, op0=OP.mult),
-               [rg(lo, 32, 64), rg("DM")], [("EF", l, l + 1)], el(32))
+            do("v", lambda e: e.tensor_scalar(out=T.EF[:, l:512:16], in0=T[lo][:, 64:96], scalar1=ap(rg("DM", l, l + 1)), scalar2=None, op0=OP.mult),
+               [rg(lo, 64, 96), rg("DM")], [("EF", l, l + 1)], el(32))
         for l in range(16):
             spread(l)
-        mm(rg("RL"), [(rg("BLK"), rg("EF"), 128)])
-        act(rg("BROW"), rg("RL"))
-        cp(rg("FG"), rg(lo, 0, 32))
-        gat(rg("NROW"), rg("BROW"), rg("FG"))
+        spreads[:] = [mm(rg("RL"), [(rg("BLK"), rg("EF"), 128)])][:BX]
+        cp(rg("BROW"), rg("RL"))
+        gat(rg("NROW"), rg("BROW"), rg("AS%d" % (RO - 2), 0, 32))
         mm(rg("RL", 0, 32), [(rg("SEL16"), rg("NROW"), None)])
-        cp(rg("LA"), rg("RL", 0, 32))
-        send("mB")
+        cp(rg(lo, 96, 128), rg("RL", 0, 32))
 
-    def take_nurses(t):
-        cp(rg("HF"), rg("HU%d" % t))
-        cp(rg("VT", 256, 512), rg("HU%d" % t))
+    def take_nurses(t, a, b):
+        for o in (rg("HF", a, b), rg("VT", 256 + a, 256 + b)):
+            cp(o, rg("HU%d" % t, a, b), after=tuple(swept) if t else ())
 
     def take_flyers(t, a, b):
-        cp(rg("AF", a, b), rg("AU%d" % t, a, b))
+        cp(rg("AF", a, b), rg("AU%d" % t, 32 + a, 32 + b), after=tuple(wiped) if t else ())
         tt(rg("DD", a, b) if t < RO - 1 else rg("VT", a, b), rg("VT", 256 + a, 256 + b), rg("AF", a, b), OP.subtract)
 
     def take_lists(t):
         if t:
-            cp(rg("FU%d" % t), rg("LS%d" % t, 0, 16))
+            cp(rg("LS%d" % t, 0, 32), rg("AU%d" % t, 0, 32), after=tuple(nurses))
         tt(rg("DFG"), rg("LS%d" % t, 16, 32), rg("LS%d" % t, 0, 16), OP.subtract)
         if t < RO - 1:
             cp(rg("FH"), rg("LS%d" % t, 0, 16))
-            gat(rg("FB"), rg("BITS", 0, 512), rg("FU%d" % t), "s")
+            gat(rg("FB"), rg("BITS", 0, 512), rg("AU%d" % t, 0, 16), "s")
         else:
-            cp(rg("AL"), rg("LB"))
-            tt(rg("DAN"), rg("LB", 0, 16), rg("LB", 16, 32), OP.subtract)
+            cp(rg("AL"), rg("LS%d" % t, 96, 128), after=(flyers[LATE],))
+            tt(rg("DAN"), rg("LS%d" % t, 96, 112), rg("LS%d" % t, 112, 128), OP.subtract)
 
     def decide(t, c):
         a, b = CH[c]
         n = b - a
         z, r, sr = [("Z%d" % c, o, o + n) for o in (0, 128, 256)]
         sw = rg("SW", a, b)
-        f = rg("FU%d" % t, a // 16, b // 16)
+        f = rg("AU%d" % t, a // 16, b // 16)
         if t < RO - 1:
             ts(sw, z, rg("TH2"), OP.is_gt, -SH, OP.add)
-            mm(r, [(rg("BR"), sw, 128)])
-            mm(sr, [(rg("BLK"), sw, 128)])
-            o = 128 * (c % 2)
-            xs, xd = ("VT", o, o + n), ("VT", o + 64, o + 64 + n)
-            i = ts(xs, r, BIG, OP.add, BIG, OP.not_equal)
-            act(rg("QS", a, b), sr, AF.Identity, 8192.0, 8192.0 * (16 * SH - 8.5), after=(i,))
+            last[:] = [mm(r, [(rg("BR"), sw, 128)]), mm(sr, [(rg("BLKQ"), sw, 128), (rg("ONE"), rg("CQ", 0, n), 1)])]
+            xs = xd = ("VT", a, b)
+            ts(xs, r, BIG, OP.add, BIG, OP.not_equal)
             tt(xd, xs, rg("DD", a, b), OP.mult)
             tt(rg("HN", a, b), rg("HF", a, b), xd, OP.subtract)
             cp(rg("HS%d" % t, a, b), rg("HN", a, b))
@@ -474,74 +519,87 @@ def rank_program(g, core, T, topo):
                 if hi == b:
                     send("mH%d_%d" % (t, j))
             tt(rg("AN", a, b), rg("AF", a, b), xd, OP.add)
-            sca(rg("VW%d" % t), f, rg("AN", a, b), rg("QS", a, b), OP.add)
+            tt(rg("QS", a, b), rg("AN", a, b), sr, OP.add)
+            sca(rg("VW%d" % t), f, rg("QS", a, b), q="s")
         else:
             ts(sw, z, rg("TH2"), OP.is_gt)
-            mm(sr, [(rg("BLK"), sw, 128)])
-            act(rg("FLG", a, b), sr, AF.Sign, 1.0, -8.5)
-            sca(rg("VF"), f, rg("FLG", a, b))
+            last[:] = [mm(sr, [(rg("BLK"), sw, 128)])]
+            if QF == "s":
+                act(rg("QS", a, b), sr, AF.Identity, 8192.0, -8192.0 * 8.5)
+                sca(rg("VW%d" % t), f, rg("QS", a, b), q="s")
+            else:
+                ts(rg("FLG", a, b), sr, 9.0, OP.is_ge)
             tt(rg("XDF", a, b), rg("VT", a, b), sw, OP.mult)
-            sca(rg("YC"), rg("AL", a // 16, b // 16), rg("AF", a, b), rg("XDF", a, b), OP.add)
-            sca(rg("YC"), rg("AL", 16 + a // 16, 16 + b // 16), rg("HF", a, b), rg("XDF", a, b), OP.subtract)
+            for lo, hi in YS:
+                if hi == b:
+                    if QF == "v":
+                        sca(rg("VF"), rg("AU%d" % t, lo // 16, hi // 16), rg("FLG", lo, hi))
+                    sca(rg("YC"), rg("AL", lo // 16, hi // 16), rg("AF", lo, hi), rg("XDF", lo, hi), OP.add)
+                    sca(rg("YC"), rg("AL", 16 + lo // 16, 16 + hi // 16), rg("HF", lo, hi), rg("XDF", lo, hi), OP.subtract)
 
     def bits(t):
-        n = CH[0][1]
-        s, x = ("SLB", 64, 64 + n), ("SLB", 0, 16)
-        i = mm(s, [(rg("WB"), rg("SW", a, b), 128) for a, b in CH])
+        s = ("SLB", 64, 128)
+        i = mm(s, [(rg("WB"), rg("SW", a, a + 64), 128) for a in range(0, P, 64)], tuple(last))
         red(rg("TS"), s)
         ts(rg("RI"), rg("TS"), FRAC, OP.add)
         ts(rg("HB"), rg("RI"), rg("TS"), OP.subtract, rg("CC"), OP.is_le)
         x = ("RL", 0, 16)
-        if t < RO - 1:
-            mm(x, [(rg("IDN"), rg("ILB"), 128), (rg("IDN"), rg("EB"), 128), (rg("SEL16"), rg("SW"), None)], (i,))
-        else:
+        if t == RO - 1:
             mm(x, [(rg("SEL"), rg("SW"), None)], (i,))
         return x
 
-    def store(x):
-        tt(rg("MW"), x, rg("LIM"), OP.is_ge)
-        tt(rg("XW"), x, rg("MW"), OP.subtract)
-        ts(rg("XC"), rg("XW"), 16.0, OP.mult)
-        sca(rg("X"), rg("XC"), rg("PFB"))
+    def store(a, b):
+        c, d = a // 16, b // 16
+        x = ("RL", c, d)
+        mm(x, [(rg("IDN"), rg("ILB", c, d), 128), (rg("IDN"), rg("EB", c, d), 128), (rg("SEL16"), rg("SW", a, b), None)])
+        tt(rg("MW", c, d), x, rg("LIM", c, d), OP.is_ge)
+        tt(rg("XW", c, d), x, rg("MW", c, d), OP.subtract)
+        ts(rg("XC", c, d), rg("XW", c, d), 16.0, OP.mult)
+        sca(rg("X"), rg("XC", c, d), rg("PFB", a, b))
+        stored[:] = [len(ops) - 1][:SF]
 
     def partners(t, x):
         e = ("SLB", 0, 16)
         tt(rg("LOW"), x, rg("LF"), OP.is_lt)
-        ts(rg("RH"), rg("FB"), rg("HB"), OP.mult)
+        scaled(rg("RH"), rg("FB"), rg("HB"), QR)
         mm(e, [(rg("IDN"), rg("FH"), 128), (rg("K1024"), rg("LOW"), 128), (rg("SEL"), rg("RH"), None)])
         ts(rg("EU"), e, 512.0, OP.min)
 
         def part(a, b):
             o, off = rg("WI", a, b), rg("EU", a // 16, b // 16)
             do("v", lambda e: e.tensor_tensor(out=ap(o), in0=ap(rg("VW%d" % t)).indirect(ap(off)), in1=T.AN[:, a:b], op=OP.max),
-               [rg("VW%d" % t), off, rg("AN", a, b)], [o], 0.05 + (b - a) * GA * CY)
+               [rg("VW%d" % t), off, rg("AN", a, b)], [o], 0.05 + (b - a) * GA * CY, tuple(stored))
         for j, (a, b) in enumerate(AM):
             part(a, b)
             ts(rg("WJ", a, b), rg("WI", a, b), 4095, OP.bitwise_and)
-            cp(rg("AS%d" % t, a, b), rg("WJ", a, b))
+            cp(rg("AS%d" % t, 32 + a, 32 + b), rg("WJ", a, b))
             send("mA%d_%d" % (t, j))
 
     def sites(t, out):
         ls = "LS%d" % t
         row = rg("VF")
-        if t < RO - 1:
+        if t < RO - 1 or QF == "s":
             row = rg("VB")
             act(row, rg("VW%d" % t, 0, 512), AF.Sign)
         z = "Z0"
         mm((z, 384, 416), [(rg("SEL"), row, None)])
-        ts(rg(ls, 64, 96), (z, 384, 416), 0.0, OP.is_gt)
-        ts(rg("LH"), rg("BITS", 512, 640), rg("HB"), OP.mult)
+        if QT[t] == "s":
+            act(rg(ls, 32, 64), (z, 384, 416), AF.Relu, 0.0625)
+        else:
+            ts(rg(ls, 32, 64), (z, 384, 416), 0.0, OP.is_gt)
+        scaled(rg("LH"), rg("BITS", 512, 640), rg("HB"), "s")
         z = "Z1"
         mm((z, 384, 512), [(rg("ONE"), rg("LH"), 4)])
         mm((z, 320, 324), [(rg("IDN"), rg("J4", 0, 4), 128), (rg("LH"), rg("RP2", 0, 4), 9)])
         cp(rg("HLU"), (z, 320, 324))
         tt(rg("PM"), (z, 384, 512), rg("NCM"), OP.is_equal)
-        gat(rg("GXL"), rg(ls, 32, 96), rg("HLU"))
-        mm((z, 320, 384), [(rg("PM"), rg("GXL"), 128)])
-        tt(rg("BO"), (z, 352, 384), rg(ls, 64, 96), OP.mult)
-        tt(rg("BD"), (z, 320, 352), rg(ls, 32, 64), OP.subtract)
-        tt(rg("BE"), rg("BO"), rg("BD"), OP.mult)
-        tt(out, rg("BE"), rg(ls, 32, 64), OP.add)
+        for o in (32, 0):
+            gat(rg("GXL", o, o + 32), rg(ls, 32 + o, 64 + o), rg("HLU", 0, 2), QT[t])
+            mm((z, 320 + o, 352 + o), [(rg("PM"), rg("GXL", o, o + 32), 128)])
+        tt(rg("BD"), (z, 352, 384), rg(ls, 64, 96), OP.subtract)
+        tt(rg("BO"), rg("BD"), rg(ls, 32, 64), OP.mult)
+        tt(rg("BE"), (z, 320, 352), rg("BO"), OP.mult)
+        tt(out, rg("BE"), rg(ls, 64, 96), OP.add)
 
     def turns(t, x):
         if t < RO - 1:
@@ -552,11 +610,12 @@ def rank_program(g, core, T, topo):
         if t < RO - 1:
             tt(rg("LO%d" % t, 0, 16), rg("LS%d" % t, 0, 16), rg("TD"), OP.add)
             tt(rg("LO%d" % t, 16, 32), rg("LS%d" % t, 16, 32), rg("TD"), OP.subtract)
+            cp(rg("AS%d" % t, 0, 32), rg("LO%d" % t, 0, 32))
         else:
             tt(rg("YF"), rg("LS%d" % t, 0, 16), rg("TD"), OP.add)
             dma("y", T.yf[:], T.YF[:], "yf", [rg("YF")], [], 2.3)
             tt(rg("TA"), rg("TL"), rg("DAN"), OP.mult)
-            tt(rg("YN"), rg("LB", 16, 32), rg("TA"), OP.add)
+            tt(rg("YN"), rg("LS%d" % t, 112, 128), rg("TA"), OP.add)
             dma("y", T.yn[:], T.YN[:], "yn", [rg("YN")], [], 2.3)
 
     start()
@@ -565,32 +624,38 @@ def rank_program(g, core, T, topo):
         for role, a, b in parts:
             frames(role, t, a, b)
             maxima(role, a, b)
+            if role == "H":
+                take_nurses(t, a, b)
+                nurses[:] = swept if t else []
+            else:
+                take_flyers(t, a, b)
+                flyers[a // 64:] = swept
             for c, (lo, hi) in enumerate(CH):
                 if a <= lo < b:
                     sums(role, c, lo, hi)
-        take_nurses(t)
-        for a, b in AM:
-            take_flyers(t, a, b)
         take_lists(t)
         for c in range(len(CH)):
             decide(t, c)
         x = bits(t)
         if t < RO - 1:
-            store(x)
-            partners(t, x)
+            for a, b in ST:
+                store(a, b)
             turns(t, x)
-            sites(t, rg("LO%d" % t, 32, 64))
-            send("mL%d" % t)
+            partners(t, x)
+            sites(t, rg("LO%d" % t, 64, 96))
             if t == RO - 2:
                 boxes()
+            send("mL%d" % t)
         else:
             dma("y", T.yc[:], T.YC[:], "yc", [rg("YC")], [], 3.4)
             sites(t, rg("YB"))
             dma("s", T.yb[:], T.YB[:], "yb", [rg("YB")], [], 2.3)
             turns(t, x)
-    for o in ops[:len(LOADS)] + [o for o in arrange(ops) if not (o["kind"] == "dma" and not o["rd"])]:
-        issue(o)
+    if not ORDER:
+        ORDER.extend(arrange(ops))
+    for i in ORDER:
+        issue(ops[i])
 
     for sem, n in list(cnt.items()) + list(total.items()):
         wait("g", sem, n, {})
-    g.wait_ge(T.sem.loc, NE * len(MSGS))
+    g.wait_ge(T.sem.loc, len(topo.engines(core, via[0])) * len(MSGS))

from concourse.mybir import AluOpType as OP, AxisListType, ActivationFunctionType as AF

P, WX, RO = 256, 4096, 3
CH = [(0, 64), (64, 128), (128, 192), (192, 256)]
HC = CH
HM = CH
AM = [(0, 128), (128, 256)]
ST = [(0, 256)]
PASSES, NV, NG, IP = 1, 10, 4, 512
YS = [(0, 192), (192, 256)]
QR, LATE, NR, BX, QI, QF = "v", 3, 1, False, "s", "s"
VG = {(t, r, 0): 32 for t in range(RO) for r in "HA"}
KB, SB, SF, QT = 1, 0, 1, "vvs"
ORDER = []
LN2 = 0.6931471805599453
FRAC = -0.5 + 2.0 ** -10
SH = 25.0 / 64
BIG = 1.5 * 2.0 ** 27
CY, GA, SC, PE, WK, HOP, FIRST, RATE = 0.00083, 1.7, 3.8, 0.00042, 0.22, 6.0, 2.0, 250e3

SCRATCH = {}


def _sb(name, cols, dtype="float32"):
    SCRATCH[name] = ("sbuf", [128, cols], dtype)


for _d, _l in (
        ("bfloat16", "X:4096 PFB:256 PNB:256 CF:4096 CN:4096 GH:4096 GA:4096 OHF:4096 OHN:4096 OAF:4096 OAN:4096 KHF:256 KHN:256 KAF:256 KAN:256 "
                     "SEL:144 NSEL:144 SEL16:144 ONE:128 BLK0:128 BLK:128 IDN:128 BR:128 K1024:128 WB0:128 WB:128 BITS:640 RP0:16 RP1:16 RP2:16 J4:16 "
                     "PW:1 PR:1 ILB:16 EB:16 SW:256 FB:256 RH:256 LOW:16 LH:128 BLKQ:128 CQ:128 VB:512 VF:512 FLG:256"),
        ("int32", "CBI:512 BSI:32 FSI:16 NBI:16 THI:1 CS:512 BI:640 BJ:640 WI:256 WJ:256"),
        ("uint16", "LU0:64 AL:32 XC:16 EU:16 HLU:4"),
        ("float16", "GROW:256 FH:16 EF:512 NROW:512"),
        ("float32", "M16:128 MB0:128 M16B:128 NCM:128 IOV:640 IC16:16 INV:512 BROW:512 HF:256 HN:256 "
                    "PM:128 GXL:64 AF:256 DD:256 AN:256 QS:256 XDF:256 YC:512 YB:32 YF:16 YN:16 VW0:528 VW1:528 VW2:512")):
    for _e in _l.split():
        _sb(_e.split(":")[0], int(_e.split(":")[1]), _d)
for _t in range(RO):
    for _n, _c, _d in [("AU", 288, "uint16"), ("HU", 256, "uint16"), ("LS", 128, "float32")]:
        _sb(_n + str(_t), _c, _d)
    if _t < RO - 1:
        for _n, _c, _d in [("AS", 288, "uint16"), ("HS", 256, "uint16"), ("LO", 128, "float32")]:
            _sb(_n + str(_t), _c, _d)
ALIAS = {}
for _k, _d, _l in (("KF", "float32", "PL:1 P2:1 NP2:1 CC:1 TH2:1 TS:1 HB:1 DM:16 IL:16 E16:16 LB0:16 LIM:16 LT:16 LF:16 "
                                     "MW:16 XW:16 TL:16 DFG:16 TD:16 DAN:16 TA:16 BO:32 BD:32 BE:32"),
                   ("KI", "int32", "EI:16 EJ:16 PI:1 PJ:1 RI:1")):
    _o = 0
    for _e in _l.split():
        ALIAS[_e.split(":")[0]] = (_k, _o, int(_e.split(":")[1]))
        _o += int(_e.split(":")[1])
    _sb(_k, _o, _d)
PS = ["Z0", "Z1", "Z2", "Z3", "VT", "PF", "SLB", "RL"]
for _n in PS:
    SCRATCH[_n] = ("psum", [128, 512], "float32")

MSGS = []
for _t in range(RO - 1):
    MSGS += [("mH%d_%d" % (_t, _c), "HS%d" % _t, "HU%d" % (_t + 1), _a, _b) for _c, (_a, _b) in enumerate(HM)]
    MSGS += [("mA%d_%d" % (_t, _c), "AS%d" % _t, "AU%d" % (_t + 1), _a and 32 + _a, 32 + _b) for _c, (_a, _b) in enumerate(AM)]
    MSGS += [("mL%d" % _t, "LO%d" % _t, "LS%d" % (_t + 1), 64, 96 if _t < RO - 2 else 128)]
LOADS = [("y", "NBI", "nb"), ("s", "PFB", "pf"), ("y", "BSI", "bs"), ("s", "PNB", "pn"), ("y", "CBI", "cb"), ("s", "FSI", "fs"), ("y", "X", "xf"), ("s", "THI", "th")]
OUTS = ["yc", "yb", "yf", "yn"]
SEMAPHORES = ["sv", "ss", "sp", "sg", "loc"] + [m[0] for m in MSGS] + ["d" + n[1] for n in LOADS] + ["d" + n for n in OUTS]


def hop(core, dst, topo, T, j):
    if topo.may_write(core, dst):
        return core
    own = [c for c in topo.cores_of(core) if T.rank_of(c) is None and topo.may_write(c, dst) and topo.die(c) == topo.die(core)][:NR]
    return own[j % len(own)]


def put(g, T, topo, src, dst, out, in_, sem):
    rid, pid = topo.addr(dst, src)
    g.remote_dma(out_ap=out, in_ap=in_, remote_sem=T.sem[sem], local_sem=T.sem.loc, pid=pid, routing_id=rid, dma_engine_mask=topo.mask(src, dst))


def relay_program(g, core, T, topo):
    for r, c in enumerate(T.cores):
        dst = T.cores[(r + 1) % len(T.cores)]
        mine = [m for j, m in enumerate(MSGS) if c in topo.cores_of(core) and hop(c, dst, topo, T, j) == core]
        for sem, _, land, a, b in mine:
            g.wait_ge(T.sem[sem], len(topo.engines(c, core)))
            put(g, T, topo, core, dst, T[land][:, a:b], T[land][:, a:b], sem)
        if mine:
            g.wait_ge(T.sem.loc, len(topo.engines(core, dst)) * len(mine))


def arrange(ops):
    n = len(ops)
    pred = [set(o["after"]) for o in ops]
    feeds = set()
    hist = {}
    for i, o in enumerate(ops):
        for group, w in ((o["rd"], False), (o["wr"], True)):
            for name, lo, hi in group:
                for j, jlo, jhi, jw in hist.get(name, []):
                    if j != i and jlo < hi and lo < jhi and (w or jw):
                        pred[i].add(j)
                        feeds.add((j, i))
        for group, w in ((o["rd"], False), (o["wr"], True)):
            for name, lo, hi in group:
                old = hist.get(name, [])
                if w:
                    old = [r for r in old if not (r[1] >= lo and r[2] <= hi)]
                hist[name] = old + [(i, lo, hi, w)]
    succ = [[] for _ in ops]
    for i in range(n):
        for j in pred[i]:
            succ[j].append(i)

    def lag(i, j):
        return 0.0 if ops[i]["q"] == ops[j]["q"] and (ops[i]["q"] == "p" or (i, j) not in feeds) else WK
    rank = [0.0] * n
    for i in range(n - 1, -1, -1):
        rank[i] = ops[i]["cost"] + max([rank[j] + lag(i, j) for j in succ[i]] + [0.0])
    banks = [set(r[0] for r in o["rd"] + o["wr"] if r[0] in PS) for o in ops]

    def place(order, back):
        start = [0.0] * n
        taken = {}
        for i in order:
            o = ops[i]
            hold, q = o["hold"], o["q"]
            if back:
                st = max([start[j] + lag(i, j) + o["cost"] - hold for j in succ[i]] + [o["cost"] - hold])
            else:
                st = max([start[j] + ops[j]["cost"] + lag(j, i) for j in pred[i]] + [0.0])
            moved = hold > 0
            while moved:
                moved = False
                for name in [q] + sorted(banks[i]):
                    for lo, hi, who in taken.get(name, []):
                        gap = 0.0 if who == q else WK
                        if (name == q or who != q) and lo - gap < st + hold - 1e-9 and st < hi + gap - 1e-9:
                            st, moved = hi + gap, True
            if hold:
                for name in [q] + sorted(banks[i]):
                    taken.setdefault(name, []).append((st, st + hold, q))
                    taken[name].sort()
            start[i] = st + hold if back else st
        return start

    start = place(sorted(range(n), key=lambda i: (-rank[i], i)), False)
    best = None
    for _ in range(PASSES):
        back = place(sorted(range(n), key=lambda i: (-start[i] - ops[i]["hold"], -i)), True)
        start = place(sorted(range(n), key=lambda i: (-1e9 if ops[i]["first"] else -back[i], i)), False)
        end = max(start[i] + ops[i]["cost"] for i in range(n))
        if best is None or end < best[0]:
            best = (end, start)
    return sorted(range(n), key=lambda i: (-1.0 if ops[i]["first"] else best[1][i], i))


def rank_program(g, core, T, topo):
    rank = T.rank_of(core)
    if rank is None:
        relay_program(g, core, T, topo)
        return
    nxt = T.cores[(rank + 1) % len(T.cores)]
    via = [hop(core, nxt, topo, T, j) for j in range(len(MSGS))]
    via = [nxt if c == core else c for c in via]
    NE = len(topo.engines(hop(T.cores[rank - 1], core, topo, T, 0), core))

    Q = {"v": g.vector, "s": g.scalar, "p": g.tensor, "g": g, "y": g.sync}
    QS = {"v": "sv", "s": "ss", "p": "sp", "g": "sg"}
    cnt = {"sv": 0, "ss": 0, "sp": 0, "sg": 0}
    known = {q: {} for q in Q}
    acc = {}
    total = {}
    ops, table = [], []
    read, swept, last, nurses, flyers, wiped, spreads, summed, stored = [], [], [], [], [], [], [], [], []

    def wait(q, sem, val, know):
        k = known[q]
        if k.get(sem, 0) < val:
            Q[q].wait_ge(T.sem[sem], val)
            k[sem] = val
            for s2, v2 in know.items():
                if k.get(s2, 0) < v2:
                    k[s2] = v2

    def deps(q, reads, writes, dma=False):
        need = {}
        for group, w in ((reads, False), (writes, True)):
            for name, lo, hi in group:
                ps = name in PS
                for r in acc.get(name, []):
                    same = r[3] == q and not r[6] and not dma
                    if (r[0] >= hi or r[1] <= lo) and (same or not ps):
                        continue
                    if not (w or r[2] or (ps and not same)):
                        continue
                    if same and q == "p":
                        continue
                    if r[4] not in need or need[r[4]][0] < r[5]:
                        need[r[4]] = (r[5], r[7])
        for sem in sorted(need, key=lambda s: -len(need[s][1])):
            wait(q, sem, need[sem][0], need[sem][1])

    def note(q, reads, writes, sem, val, dma):
        know = dict(known[q])
        for group, w in ((reads, False), (writes, True)):
            for name, lo, hi in group:
                old = acc.get(name, [])
                if name in PS:
                    keep = [r for r in old if r[3] == q and not (r[0] >= lo and r[1] <= hi and (w or not r[2]))]
                elif w:
                    keep = [r for r in old if not (r[0] >= lo and r[1] <= hi)]
                else:
                    keep = [r for r in old if not (r[0] >= lo and r[1] <= hi and r[3] == q and not r[2] and not r[6] and not dma)]
                acc[name] = keep + [(lo, hi, w, q, sem, val, dma, know)]

    def add(kind, q, fns, rd, wr, cost, hold=None, after=(), extra=None):
        ops.append({"kind": kind, "q": q, "fns": fns, "rd": rd, "wr": wr, "cost": cost, "hold": cost if hold is None else hold, "after": after, "extra": extra,
                    "first": kind == "dma" and not rd})
        return len(ops) - 1

    def do(q, fns, rd, wr, cost, after=()):
        return add("do", q, fns if isinstance(fns, list) else [fns], rd, wr, cost, None, after)

    def dma(q, out, in_, name, rd, wr, cost):
        add("dma", q, [lambda e: e.dma_start(out=out, in_=in_)], rd, wr, cost, 0.1, (), "d" + name)

    def send(sem):
        _, src, land, a, b = [m for m in MSGS if m[0] == sem][0]
        more = FIRST if sem == MSGS[0][0] else 0.0
        i = add("send", "g", None, [(src, a, b)], [("SENDQ", 0, 1)], 1.0 + more, 1.0 + more, (), sem)
        add("land", "r", None, [], [(land, a, b)], HOP - 1.0 + more, 0.0, (i,), sem)

    def issue(o):
        q = o["q"]
        if o["kind"] == "do":
            deps(q, o["rd"], o["wr"])
            for fn in o["fns"]:
                cnt[QS[q]] += 1
                fn(Q[q]).then_inc(T.sem[QS[q]], 1)
            note(q, o["rd"], o["wr"], QS[q], cnt[QS[q]], False)
        elif o["kind"] == "dma":
            deps(q, o["rd"], o["wr"], True)
            o["fns"][0](Q[q]).then_inc(T.sem[o["extra"]], 16)
            total[o["extra"]] = 16
            note(q, o["rd"], o["wr"], o["extra"], 16, True)
        elif o["kind"] == "send":
            m = [m for m in MSGS if m[0] == o["extra"]][0]
            deps("g", o["rd"], [])
            put(g, T, topo, core, via[MSGS.index(m)], T[m[2]][:, m[3]:m[4]], T[m[1]][:, m[3]:m[4]], m[0])
        else:
            land, a, b = o["wr"][0]
            acc.setdefault(land, []).append((a, b, True, "r", o["extra"], NE, True, {}))
            total[o["extra"]] = NE

    def rg(name, a=0, b=None):
        if name in ALIAS:
            k, o, w = ALIAS[name]
            return (k, o + a, o + (w if b is None else b))
        return (name, a, SCRATCH[name][1][1] if b is None else b)

    def ap(x):
        return T[x[0]][:, x[1]:x[2]]

    def val(s):
        return ap(s) if isinstance(s, tuple) else s

    def two(x):
        return SCRATCH[x[0]][0] == "sbuf" and SCRATCH[x[0]][2] in ("bfloat16", "float16", "uint16")

    def el(n, f=1.0):
        return max(64, n * f) * CY

    def tt(o, x, y, op):
        f = 1.0 if x[0] in PS or y[0] in PS else 2.0
        return do("v", lambda e: e.tensor_tensor(out=ap(o), in0=ap(x), in1=ap(y), op=op), [x, y], [o], el(o[2] - o[1], f))

    def ts(o, x, s1, op0, s2=None, op1=None):
        rd = [x] + [s for s in (s1, s2) if isinstance(s, tuple)]
        c = el(o[2] - o[1], 0.5 if two(o) and two(x) else 1.0)
        if op1 is None:
            return do("v", lambda e: e.tensor_scalar(out=ap(o), in0=ap(x), scalar1=val(s1), scalar2=None, op0=op0), rd, [o], c)
        return do("v", lambda e: e.tensor_scalar(out=ap(o), in0=ap(x), scalar1=val(s1), scalar2=val(s2), op0=op0, op1=op1), rd, [o], c)

    def cp(o, x, out=None, in_=None, n=None, after=()):
        w, r = out if out is not None else ap(o), in_ if in_ is not None else ap(x)
        do("v", lambda e: e.tensor_copy(out=w, in_=r), [x], [o], el(n or x[2] - x[1], 0.5 if two(o) and two(x) else 1.0), after)

    def act(o, x, func=AF.Copy, scale=1.0, bias=None, out=None, n=None, after=()):
        w = out if out is not None else ap(o)
        c = max(64, n or x[2] - x[1]) * CY + 0.05
        if bias is None:
            return do("s", lambda e: e.activation(w, ap(x), func, scale=scale), [x], [o], c, after)
        return do("s", lambda e: e.activation(w, ap(x), func, bias=bias, scale=scale), [x], [o], c, after)

    def scaled(o, x, col, q):
        if q == "v":
            ts(o, x, col, OP.mult)
        else:
            do("s", lambda e: e.activation(ap(o), ap(x), AF.Copy, scale=ap(col)), [x, col], [o], (x[2] - x[1]) * CY + 0.05)

    def red(o, x):
        do("v", lambda e: e.tensor_reduce(ap(o), ap(x), AxisListType.X, OP.add), [x], [o], el(x[2] - x[1]))

    def fill(o, c):
        do("v", lambda e: e.memset(ap(o), c), [], [o], el(o[2] - o[1], 0.5 if two(o) else 1.0))

    def gat(o, win, off, q="v", after=()):
        c = 0.06 + (o[2] - o[1]) * GA * CY
        if q == "v":
            do("v", lambda e: e.tensor_copy(out=ap(o), in_=ap(win).indirect(ap(off))), [win, off], [o], c)
        else:
            return do("s", lambda e: e.activation(ap(o), ap(win).indirect(ap(off)), AF.Copy), [win, off], [o], c, after)

    def sca(win, off, x, y=None, op=None, q="v"):
        c = 0.05 + (x[2] - x[1]) * SC * CY
        if q == "s":
            do("s", lambda e: e.activation(ap(win).indirect(ap(off)), ap(x), AF.Silu), [x, off], [win], c + (0.0 if table else 1.5))
            table.append(1)
        elif y is None:
            do("v", lambda e: e.tensor_copy(out=ap(win).indirect(ap(off)), in_=ap(x)), [x, off], [win], c)
        else:
            do("v", lambda e: e.tensor_tensor(out=ap(win).indirect(ap(off)), in0=ap(x), in1=ap(y), op=op), [x, y, off], [win], c)

    def mm(o, terms, after=(), whole=False):
        fl, rd = [], []
        for l, r, kp in terms:
            rd += [l, r]
            if kp is None:
                fl += [(T[l[0]][:, 15 - k:143 - k], T[r[0]][:, r[1] + k:r[2]:16]) for k in range(16)]
            else:
                fl.append((T[l[0]][0:kp, l[1]:l[2]], T[r[0]][0:kp, r[1]:r[2]]))

        def one(i):
            return lambda e: e.matmul(ap(o), fl[i][0], fl[i][1], i == 0, i == len(fl) - 1)
        return do("p", [one(i) for i in range(len(fl))], rd, [o], len(fl) * max(64, o[2] - o[1]) * PE, after)

    def aff(o, x, pat, op, fillv, base, cm, out=None):
        w = out if out is not None else ap(o)
        do("g", lambda e: e.affine_select(w, ap(x), pat, op, fillv, base, cm), [x], [o], 0.17 + 2 * (x[2] - x[1]) * CY)

    def iota(o, pat, base, cm, flag=True):
        do("g", (lambda e: e.iota(ap(o), pat, base, cm, allow_small_or_imprecise_dtypes=True)) if flag else (lambda e: e.iota(ap(o), pat, base, cm)),
           [], [o], 0.13 + 2 * (o[2] - o[1]) * CY)

    def start():
        size = 0
        for q, n, src in LOADS:
            size += 128 * SCRATCH[n][1][1] * (2 if two(rg(n)) else 4)
            dma(q, T[n][:], T[src][:], n, [], [rg(n)], 2.2 + size / RATE)
        for n, c in (("ONE", 1.0), ("SEL", 0.0), ("CQ", 8192.0 * (16 * SH - 8.5))):
            fill(rg(n), c)
        for n, c in (("VW0", -16384), ("VW1", -16384), ("VW2" if QF == "s" else "VF", -1)):
            iota(rg(n), [[0, rg(n)[2]]], c, 0)
        aff(rg("BLK0"), rg("ONE"), [[-16, 8], [0, 16]], OP.is_ge, 0.0, 0, 1)
        aff(rg("BLK"), rg("BLK0"), [[16, 8], [0, 16]], OP.is_ge, 0.0, 15, -1)
        aff(rg("IDN"), rg("ONE"), [[-1, 128]], OP.is_equal, 0.0, 0, 1)
        cp(rg("SEL"), rg("BLK"), T.SEL[:, 15:143:16], T.BLK[:, 0:128:16], 8)
        ts(rg("NSEL"), rg("SEL"), -1.0, OP.mult)
        ts(rg("SEL16"), rg("SEL"), 0.0625, OP.mult)
        ts(rg("K1024"), rg("IDN"), 16.0, OP.mult)
        tt(rg("BR"), rg("K1024"), rg("BLK"), OP.add)
        ts(rg("K1024"), rg("IDN"), 1024.0, OP.mult)
        ts(rg("BLKQ"), rg("BLK"), 8192.0, OP.mult)
        cp(rg("LU0", 48, 64), rg("NBI"))
        gat(rg("HU0"), rg("CBI"), rg("LU0", 48, 64))
        cp(rg("LU0", 0, 32), rg("BSI"))
        gat(rg("CS"), rg("CBI"), rg("LU0", 0, 32))
        cp(rg("LU0", 32, 48), rg("FSI"))
        cp(rg("AU0", 0, 16), rg("FSI"))
        gat(rg("AU0", 32, 288), rg("CS"), rg("LU0", 32, 48))
        for j in range(32):
            c, src, k = ("CF", "PFB", j) if j < 16 else ("CN", "PNB", j - 16)
            if j < NV:
                cp((c, k, k + 1), rg(src), T[c][:, k:4096:16], T[src][:, :])
            elif j < 32 - NG:
                act((c, k, k + 1), rg(src), out=T[c][:, k:4096:16])
            else:
                aff((c, k, k + 1), rg(src), [[0, P]], OP.is_ge, 0.0, 0, 0, T[c][:, k:4096:16])
        iota(rg("PI"), [[0, 1]], 0, 1, False)
        iota(rg("M16"), [[0, 8], [1, 16]], 0, 0)
        iota(rg("IC16"), [[16, 16]], 0, 0)
        iota(rg("IOV", 0, 512), [[1, 512]], 1024, 0)
        iota(rg("IOV", 512, 640), [[0, 8], [17, 16]], 0, 0)
        ts(rg("PJ"), rg("PI"), 15, OP.bitwise_and)
        cp(rg("PL"), rg("PJ"))
        ts(rg("DM"), rg("M16", 0, 16), rg("PL"), OP.is_equal)
        ops[act(rg("PW"), rg("PL"), AF.Exp, -LN2)].update(cost=1.4, hold=1.4)
        act(rg("PR"), rg("PL"), AF.Exp, LN2)
        act(rg("WB"), rg("M16"), AF.Exp, -LN2)
        aff(rg("WB0"), rg("WB"), [[0, 8], [1, 16]], OP.is_ge, 0.0, -1, 0)
        aff(rg("WB"), rg("WB0"), [[0, 8], [-1, 16]], OP.is_ge, 0.0, 8, 0)
        ts(rg("WB"), rg("WB"), 0.5, OP.mult)
        ts(rg("P2"), rg("PL"), 9.0, OP.is_lt, rg("PR"), OP.mult)
        ts(rg("NP2"), rg("P2"), -2.0, OP.mult)
        ts(rg("CC"), rg("PL"), 1.0, OP.min, -0.5, OP.mult)
        ts(rg("BI"), rg("IOV"), rg("PW"), OP.mult, FRAC, OP.add)
        ts(rg("BJ"), rg("BI"), 1, OP.bitwise_and)
        ts(rg("BITS"), rg("BJ"), rg("NP2"), OP.mult, rg("P2"), OP.add)
        ts(rg("TH2"), rg("THI"), 0.5, OP.mult)
        aff(rg("MB0"), rg("M16"), [[-16, 8], [0, 16]], OP.is_ge, 99.0, 0, 1)
        aff(rg("M16B"), rg("MB0"), [[16, 8], [0, 16]], OP.is_ge, 99.0, 15, -1)
        ts(rg("NCM"), rg("M16B"), -1.0, OP.mult, rg("PL"), OP.add)
        iota(rg("RP0", 0, 4), [[0, 2], [-2, 2]], 1, 0)
        aff(rg("RP1", 0, 4), rg("RP0", 0, 4), [[0, 4]], OP.is_equal, 1.0, -8, 1)
        aff(rg("RP0", 0, 4), rg("RP1", 0, 4), [[0, 4]], OP.is_ge, 0.0, -4, 1)
        ts(rg("RP2", 0, 4), rg("RP0", 0, 4), 0.0625, OP.mult)
        ts(rg("J4", 0, 4), rg("IC16", 0, 4), rg("PL"), OP.add)
        ts(rg("IL"), rg("IC16"), rg("PL"), OP.add)
        cp(rg("ILB"), rg("IL"))
        mm(rg("RL", 0, 16), [(rg("SEL"), rg("PFB"), None)])
        cp(rg("EI"), rg("RL", 0, 16))
        ts(rg("EJ"), rg("EI"), 15, OP.bitwise_and)
        ts(rg("E16"), rg("EJ"), 0.0625, OP.mult)
        ts(rg("EB"), rg("E16"), SH, OP.add)
        tt(rg("LB0"), rg("IL"), rg("E16"), OP.add)
        ts(rg("LIM"), rg("IL"), 1.0, OP.add)
        ts(rg("LT"), rg("LB0"), 4.5 / 16, OP.add)
        ts(rg("LF"), rg("LB0"), 8.5 / 16, OP.add)
        cp(rg("LS0", 0, 16), rg("FSI"))
        cp(rg("LS0", 64, 96), rg("BSI"))
        for a in range(0, 512, IP):
            sca(rg("INV"), rg("LU0", a // 16, (a + IP) // 16), rg("IOV", a, a + IP), q=QI)
        gat(rg("GROW"), rg("INV"), rg("LU0", 48, 64))
        mm(rg("RL", 16, 32), [(rg("SEL16"), rg("GROW"), None)])
        ts(rg("LS0", 16, 32), rg("RL", 16, 32), -1024.0, OP.add)

    def frames(role, t, a, b):
        o = 32 * (role == "A")
        n = VG.get((t, role, a), 0)
        if n:
            gat(("G" + role, 16 * a, 16 * (a + n)), rg("X"), rg(role + "U%d" % t, o + a, o + a + n))
            a += n
        read[:] = [gat(("G" + role, 16 * a, 16 * b), rg("X"), rg(role + "U%d" % t, o + a, o + b), "s", tuple(read))]

    def maxima(role, a, b):
        gx = ("G" + role, 16 * a, 16 * b)
        row0 = T["G" + role][:, 16 * a:16 * b:16]

        o = 256 * (role == "A")
        kept = ("PF", o + a, o + b)
        do("p", lambda e: e.matmul(ap(kept), T.IDN[:, :], row0, True, True), [rg("IDN"), gx], [kept], max(64, b - a) * PE, tuple(spreads))

        def first(f, src):
            swept.extend([tt(("K" + role + f, a, b), kept, rg(src, a, b), OP.max)][:KB])

        def rest(f, c, lo, hi):
            o, d, x = ("O" + role + f, lo, hi), (c, lo, hi), (gx[0], lo, hi)
            swept[:] = [do("v", lambda e: e.tensor_tensor_scan(ap(o), ap(d), ap(x), 255.0, OP.min, OP.max), [x, rg(c)], [o], el(hi - lo, 0.5), tuple(swept))]
        wiped[:] = [do("v", lambda e: e.memset(row0, 255.0), [], [gx], el(b - a, 0.5))]
        first("F", "PFB")
        first("N", "PNB")
        for lo, hi in CH:
            if a <= lo < b:
                rest("F", "CF", 16 * lo, 16 * hi)
                rest("N", "CN", 16 * lo, 16 * hi)

    def sums(role, c, a, b):
        z = ("Z%d" % c, 0, b - a)

        def one(f, k, last):
            neg = (role == "H") == (f == "F")
            rhs = T["O" + role + f][:, 16 * a + k:16 * b:16] if k else T["K" + role + f][:, a:b]
            return lambda e: e.matmul(ap(z), T["NSEL" if neg else "SEL"][:, 15 - k:143 - k], rhs, role == "H" and f == "F" and k == 1, role == "A" and last)
        for f in ("F", "N"):
            rows = [one(f, k, f == "N" and k == 15) for k in range(1, 16)]
            summed[:] = [do("p", rows, [rg("NSEL"), rg("SEL"), ("O" + role + f, 16 * a, 16 * b)], [(z[0], 0, 512) if (role, f) == ("H", "F") else z],
                            15 * max(64, b - a) * PE, tuple(summed))][:SB]
            if f == "F":
                do("p", [one("F", 0, False), one("N", 0, False)], [rg("NSEL"), rg("SEL"), ("K" + role + "F", a, b), ("K" + role + "N", a, b)], [z], 2 * max(64, b - a) * PE)

    def boxes():
        lo = "LO%d" % (RO - 2)

        def spread(l):
            do("v", lambda e: e.tensor_scalar(out=T.EF[:, l:512:16], in0=T[lo][:, 64:96], scalar1=ap(rg("DM", l, l + 1)), scalar2=None, op0=OP.mult),
               [rg(lo, 64, 96), rg("DM")], [("EF", l, l + 1)], el(32))
        for l in range(16):
            spread(l)
        spreads[:] = [mm(rg("RL"), [(rg("BLK"), rg("EF"), 128)])][:BX]
        cp(rg("BROW"), rg("RL"))
        gat(rg("NROW"), rg("BROW"), rg("AS%d" % (RO - 2), 0, 32))
        mm(rg("RL", 0, 32), [(rg("SEL16"), rg("NROW"), None)])
        cp(rg(lo, 96, 128), rg("RL", 0, 32))

    def take_nurses(t, a, b):
        for o in (rg("HF", a, b), rg("VT", 256 + a, 256 + b)):
            cp(o, rg("HU%d" % t, a, b), after=tuple(swept) if t else ())

    def take_flyers(t, a, b):
        cp(rg("AF", a, b), rg("AU%d" % t, 32 + a, 32 + b), after=tuple(wiped) if t else ())
        tt(rg("DD", a, b) if t < RO - 1 else rg("VT", a, b), rg("VT", 256 + a, 256 + b), rg("AF", a, b), OP.subtract)

    def take_lists(t):
        if t:
            cp(rg("LS%d" % t, 0, 32), rg("AU%d" % t, 0, 32), after=tuple(nurses))
        tt(rg("DFG"), rg("LS%d" % t, 16, 32), rg("LS%d" % t, 0, 16), OP.subtract)
        if t < RO - 1:
            cp(rg("FH"), rg("LS%d" % t, 0, 16))
            gat(rg("FB"), rg("BITS", 0, 512), rg("AU%d" % t, 0, 16), "s")
        else:
            cp(rg("AL"), rg("LS%d" % t, 96, 128), after=(flyers[LATE],))
            tt(rg("DAN"), rg("LS%d" % t, 96, 112), rg("LS%d" % t, 112, 128), OP.subtract)

    def decide(t, c):
        a, b = CH[c]
        n = b - a
        z, r, sr = [("Z%d" % c, o, o + n) for o in (0, 128, 256)]
        sw = rg("SW", a, b)
        f = rg("AU%d" % t, a // 16, b // 16)
        if t < RO - 1:
            ts(sw, z, rg("TH2"), OP.is_gt, -SH, OP.add)
            last[:] = [mm(r, [(rg("BR"), sw, 128)]), mm(sr, [(rg("BLKQ"), sw, 128), (rg("ONE"), rg("CQ", 0, n), 1)])]
            xs = xd = ("VT", a, b)
            ts(xs, r, BIG, OP.add, BIG, OP.not_equal)
            tt(xd, xs, rg("DD", a, b), OP.mult)
            tt(rg("HN", a, b), rg("HF", a, b), xd, OP.subtract)
            cp(rg("HS%d" % t, a, b), rg("HN", a, b))
            for j, (lo, hi) in enumerate(HM):
                if hi == b:
                    send("mH%d_%d" % (t, j))
            tt(rg("AN", a, b), rg("AF", a, b), xd, OP.add)
            tt(rg("QS", a, b), rg("AN", a, b), sr, OP.add)
            sca(rg("VW%d" % t), f, rg("QS", a, b), q="s")
        else:
            ts(sw, z, rg("TH2"), OP.is_gt)
            last[:] = [mm(sr, [(rg("BLK"), sw, 128)])]
            if QF == "s":
                act(rg("QS", a, b), sr, AF.Identity, 8192.0, -8192.0 * 8.5)
                sca(rg("VW%d" % t), f, rg("QS", a, b), q="s")
            else:
                ts(rg("FLG", a, b), sr, 9.0, OP.is_ge)
            tt(rg("XDF", a, b), rg("VT", a, b), sw, OP.mult)
            for lo, hi in YS:
                if hi == b:
                    if QF == "v":
                        sca(rg("VF"), rg("AU%d" % t, lo // 16, hi // 16), rg("FLG", lo, hi))
                    sca(rg("YC"), rg("AL", lo // 16, hi // 16), rg("AF", lo, hi), rg("XDF", lo, hi), OP.add)
                    sca(rg("YC"), rg("AL", 16 + lo // 16, 16 + hi // 16), rg("HF", lo, hi), rg("XDF", lo, hi), OP.subtract)

    def bits(t):
        s = ("SLB", 64, 128)
        i = mm(s, [(rg("WB"), rg("SW", a, a + 64), 128) for a in range(0, P, 64)], tuple(last))
        red(rg("TS"), s)
        ts(rg("RI"), rg("TS"), FRAC, OP.add)
        ts(rg("HB"), rg("RI"), rg("TS"), OP.subtract, rg("CC"), OP.is_le)
        x = ("RL", 0, 16)
        if t == RO - 1:
            mm(x, [(rg("SEL"), rg("SW"), None)], (i,))
        return x

    def store(a, b):
        c, d = a // 16, b // 16
        x = ("RL", c, d)
        mm(x, [(rg("IDN"), rg("ILB", c, d), 128), (rg("IDN"), rg("EB", c, d), 128), (rg("SEL16"), rg("SW", a, b), None)])
        tt(rg("MW", c, d), x, rg("LIM", c, d), OP.is_ge)
        tt(rg("XW", c, d), x, rg("MW", c, d), OP.subtract)
        ts(rg("XC", c, d), rg("XW", c, d), 16.0, OP.mult)
        sca(rg("X"), rg("XC", c, d), rg("PFB", a, b))
        stored[:] = [len(ops) - 1][:SF]

    def partners(t, x):
        e = ("SLB", 0, 16)
        tt(rg("LOW"), x, rg("LF"), OP.is_lt)
        scaled(rg("RH"), rg("FB"), rg("HB"), QR)
        mm(e, [(rg("IDN"), rg("FH"), 128), (rg("K1024"), rg("LOW"), 128), (rg("SEL"), rg("RH"), None)])
        ts(rg("EU"), e, 512.0, OP.min)

        def part(a, b):
            o, off = rg("WI", a, b), rg("EU", a // 16, b // 16)
            do("v", lambda e: e.tensor_tensor(out=ap(o), in0=ap(rg("VW%d" % t)).indirect(ap(off)), in1=T.AN[:, a:b], op=OP.max),
               [rg("VW%d" % t), off, rg("AN", a, b)], [o], 0.05 + (b - a) * GA * CY, tuple(stored))
        for j, (a, b) in enumerate(AM):
            part(a, b)
            ts(rg("WJ", a, b), rg("WI", a, b), 4095, OP.bitwise_and)
            cp(rg("AS%d" % t, 32 + a, 32 + b), rg("WJ", a, b))
            send("mA%d_%d" % (t, j))

    def sites(t, out):
        ls = "LS%d" % t
        row = rg("VF")
        if t < RO - 1 or QF == "s":
            row = rg("VB")
            act(row, rg("VW%d" % t, 0, 512), AF.Sign)
        z = "Z0"
        mm((z, 384, 416), [(rg("SEL"), row, None)])
        if QT[t] == "s":
            act(rg(ls, 32, 64), (z, 384, 416), AF.Relu, 0.0625)
        else:
            ts(rg(ls, 32, 64), (z, 384, 416), 0.0, OP.is_gt)
        scaled(rg("LH"), rg("BITS", 512, 640), rg("HB"), "s")
        z = "Z1"
        mm((z, 384, 512), [(rg("ONE"), rg("LH"), 4)])
        mm((z, 320, 324), [(rg("IDN"), rg("J4", 0, 4), 128), (rg("LH"), rg("RP2", 0, 4), 9)])
        cp(rg("HLU"), (z, 320, 324))
        tt(rg("PM"), (z, 384, 512), rg("NCM"), OP.is_equal)
        for o in (32, 0):
            gat(rg("GXL", o, o + 32), rg(ls, 32 + o, 64 + o), rg("HLU", 0, 2), QT[t])
            mm((z, 320 + o, 352 + o), [(rg("PM"), rg("GXL", o, o + 32), 128)])
        tt(rg("BD"), (z, 352, 384), rg(ls, 64, 96), OP.subtract)
        tt(rg("BO"), rg("BD"), rg(ls, 32, 64), OP.mult)
        tt(rg("BE"), (z, 320, 352), rg("BO"), OP.mult)
        tt(out, rg("BE"), rg(ls, 64, 96), OP.add)

    def turns(t, x):
        if t < RO - 1:
            tt(rg("TL"), x, rg("LT"), OP.is_lt)
        else:
            ts(rg("TL"), x, 4.0, OP.is_le)
        tt(rg("TD"), rg("TL"), rg("DFG"), OP.mult)
        if t < RO - 1:
            tt(rg("LO%d" % t, 0, 16), rg("LS%d" % t, 0, 16), rg("TD"), OP.add)
            tt(rg("LO%d" % t, 16, 32), rg("LS%d" % t, 16, 32), rg("TD"), OP.subtract)
            cp(rg("AS%d" % t, 0, 32), rg("LO%d" % t, 0, 32))
        else:
            tt(rg("YF"), rg("LS%d" % t, 0, 16), rg("TD"), OP.add)
            dma("y", T.yf[:], T.YF[:], "yf", [rg("YF")], [], 2.3)
            tt(rg("TA"), rg("TL"), rg("DAN"), OP.mult)
            tt(rg("YN"), rg("LS%d" % t, 112, 128), rg("TA"), OP.add)
            dma("y", T.yn[:], T.YN[:], "yn", [rg("YN")], [], 2.3)

    start()
    for t in range(RO):
        parts = [("H", a, b) for a, b in HC] + [("A", a, b) for a, b in CH] if t else [(role, a, b) for a, b in CH for role in "HA"]
        for role, a, b in parts:
            frames(role, t, a, b)
            maxima(role, a, b)
            if role == "H":
                take_nurses(t, a, b)
                nurses[:] = swept if t else []
            else:
                take_flyers(t, a, b)
                flyers[a // 64:] = swept
            for c, (lo, hi) in enumerate(CH):
                if a <= lo < b:
                    sums(role, c, lo, hi)
        take_lists(t)
        for c in range(len(CH)):
            decide(t, c)
        x = bits(t)
        if t < RO - 1:
            for a, b in ST:
                store(a, b)
            turns(t, x)
            partners(t, x)
            sites(t, rg("LO%d" % t, 64, 96))
            if t == RO - 2:
                boxes()
            send("mL%d" % t)
        else:
            dma("y", T.yc[:], T.YC[:], "yc", [rg("YC")], [], 3.4)
            sites(t, rg("YB"))
            dma("s", T.yb[:], T.YB[:], "yb", [rg("YB")], [], 2.3)
            turns(t, x)
    if not ORDER:
        ORDER.extend(arrange(ops))
    for i in ORDER:
        issue(ops[i])

    for sem, n in list(cnt.items()) + list(total.items()):
        wait("g", sem, n, {})
    g.wait_ge(T.sem.loc, len(topo.engines(core, via[0])) * len(MSGS))
